import numpy as np
import ml_dtypes


def mxq(x, axis, fmt="e4m3"):
    dtype, down = {"e4m3": (ml_dtypes.float8_e4m3fn, 7), "e5m2": (ml_dtypes.float8_e5m2, 14)}[fmt]
    v = np.moveaxis(np.asarray(x, np.float32).astype(ml_dtypes.bfloat16).astype(np.float64), axis, -1)
    blocks = v.reshape(v.shape[:-1] + (-1, 32))
    amax = np.abs(blocks).max(-1, keepdims=True)
    byte = np.maximum(np.where(amax > 0, np.frexp(amax)[1] - 1 + 127, 0) - down, 1)
    scale = np.exp2(byte - 127.0)
    codes = (blocks / scale).astype(np.float32).astype(dtype).astype(np.float64)
    return np.moveaxis((codes * scale).reshape(v.shape), -1, axis)


WIDE = False


def mx_kscale(k):
    if not WIDE:
        return np.ones(k)
    levels = np.array([10, -10, 5, -5, 0])
    if k % 512:
        return np.exp2(np.random.permutation(np.resize(levels, k // 32))).repeat(32)
    a = np.empty((k // 512, 16))
    for p in range(k // 512):
        a[p, :8] = np.random.permutation(np.resize(levels, 8))
        for g in range(8):
            far = levels[np.abs(levels - a[p, g]) >= 10]
            a[p, g + 8] = far[np.random.randint(len(far))]
    return np.exp2(a.ravel()).repeat(32)


def f64(x):
    return np.asarray(x).astype(np.float64)


def striped(idx):
    return np.tile(idx.reshape(-1, 16).T, (8, 1)).astype(np.uint16)


def unstriped(offs):
    return offs[:16].T.reshape(-1).astype(np.int64)


E2M1 = np.array([0.0, 0.5, 1.0, 1.5, 2.0, 3.0, 4.0, 6.0, -0.0, -0.5, -1.0, -1.5, -2.0, -3.0, -4.0, -6.0])


def pack_weight(w, fmt):
    k, n = w.shape
    w = f64(np.asarray(w, np.float32).astype(ml_dtypes.bfloat16)).reshape(k // 32, 32, n)
    amax = np.abs(w).max(1)
    if fmt == "e4m3":
        byte = np.frexp(amax)[1] - 1 + 127 - 7
    else:
        mant, ex = np.frexp(amax / 6.0)
        byte = np.where(mant > 0.5, ex, ex - 1) + 127
    byte = np.clip(np.where(amax > 0, byte, 1), 1, 254)
    scaled = (w * np.exp2(127.0 - byte)[:, None, :]).reshape(k, n).astype(np.float32)
    by_word = np.ascontiguousarray(scaled.reshape(k // 512, 128, 4, n).transpose(0, 1, 3, 2))
    if fmt == "e4m3":
        words = by_word.astype(ml_dtypes.float8_e4m3fn).view(np.uint8)
    else:
        c = by_word.astype(ml_dtypes.float4_e2m1fn).view(np.uint8) & 0xF
        words = (c[..., 0::2] | (c[..., 1::2] << 4)).reshape(k // 512, 128, 2 * n)
    return np.ascontiguousarray(words), np.ascontiguousarray(byte.astype(np.uint8).reshape(k // 512, 16, n))


def unpack_weight(words, scales, fmt):
    g, _, n = scales.shape
    words = np.ascontiguousarray(words).reshape(g, 128, n, -1)
    if fmt == "e4m3":
        vals = words.view(ml_dtypes.float8_e4m3fn).astype(np.float64)
    else:
        nib = np.empty((g, 128, n, 4), np.uint8)
        nib[..., 0::2] = words & 0xF
        nib[..., 1::2] = words >> 4
        vals = E2M1[nib]
    vals = vals * np.repeat(np.exp2(scales.astype(np.float64) - 127.0), 8, axis=1)[..., None]
    return vals.transpose(0, 1, 3, 2).reshape(g * 512, n)


def pack_table(v):
    words, scales = pack_weight(v, "e4m3")
    return np.concatenate([words.reshape(words.shape[0], -1), scales.reshape(scales.shape[0], -1)], axis=1)


def unpack_table(tab):
    g, t = tab.shape[0], tab.shape[1] // 528
    return unpack_weight(tab[:, :512 * t].reshape(g, 128, t, 4), tab[:, 512 * t:].reshape(g, 16, t), "e4m3")


G, K, M, T, S = 3, 1024, 256, 4096, 512


def setup_inputs():
    n = np.random.standard_normal
    s = mx_kscale(K)[:, None]
    return {
        "tab": pack_table(n((K, T)) * s),
        "w": (n((K, M)) / np.sqrt(K) / s).astype(np.float32),
        "offs": striped(np.concatenate([np.random.permutation(T)[:S] for _ in range(G)])),
    }


def reference(tab, w, offs):
    tab_ = unpack_table(tab)[:, unstriped(offs).reshape(G, S)].sum(1)
    w_ = mxq(f64(w), 0, "e4m3")
    y = tab_.T @ w_
    return y

@@ -1,0 +1,126 @@
+from contextlib import ExitStack
+
+import concourse.mybir as mybir
+
+G, K, M, T, S = 3, 1024, 256, 4096, 512
+FLOPS = 2 * G * K * M * S
+
+F32 = mybir.dt.float32
+BF16 = mybir.dt.bfloat16
+I32 = mybir.dt.int32
+U32 = mybir.dt.uint32
+U16 = mybir.dt.uint16
+U8 = mybir.dt.uint8
+FP8X4 = mybir.dt.float8_e4m3fn_x4
+
+P = 128
+PACK = 4
+K_PASS = P * PACK
+PASSES = K // K_PASS
+N_LIST = G * S
+PER_COL = 16
+WORD_BYTES = K_PASS * T
+BLOCKS = K_PASS // 32
+SPLIT = T // 2
+HW_MOVES = 6
+
+
+def tile_list_tabbag_tm_none_kernel(tc, tab, w, offs, out):
+    nc = tc.nc
+    with ExitStack() as ctx:
+        keep = ctx.enter_context(tc.tile_pool(name="keep", bufs=1))
+        psum = ctx.enter_context(tc.psum_pool(name="psum", bufs=1))
+
+        offsets = keep.tile([P, N_LIST // PER_COL], U16, name="offsets")
+        tab_scales = keep.tile([P, T], U8, name="tab_scales", align_bytes=64)
+        tab_words = [keep.tile([P, T], I32, name=f"tab_words{a}", align_bytes=64) for a in range(PASSES)]
+        w_raw = [keep.tile([P, PACK, M], F32, name=f"w_raw{a}", align_bytes=64) for a in range(PASSES)]
+        w_codes = [keep.tile([P, M], U32, name=f"w_codes{a}", align_bytes=64) for a in range(PASSES)]
+        w_scales = [keep.tile([P, M], U8, name=f"w_scales{a}", align_bytes=64) for a in range(PASSES)]
+        picked_scales = keep.tile([P, N_LIST], U8, name="picked_scales", align_bytes=64)
+        planes = [keep.tile([P, N_LIST], U8, name=f"planes{a}", align_bytes=64) for a in range(PASSES)]
+
+        def words_in_hbm(a):
+            return tab[a, 0:WORD_BYTES].rearrange("(p b) -> p b", p=P).bitcast(I32)
+
+        def w_in_hbm(a):
+            return w[a * K_PASS : (a + 1) * K_PASS, :].rearrange("(p i) n -> p i n", i=PACK)
+
+        nc.sync.dma_start(offsets[:], offs)
+        for a in range(PASSES):
+            nc.sync.dma_start(
+                tab_scales[BLOCKS * a : BLOCKS * (a + 1), :].bitcast(I32),
+                tab[a, WORD_BYTES : WORD_BYTES + BLOCKS * T].rearrange("(q t) -> q t", q=BLOCKS).bitcast(I32),
+            )
+        nc.sync.dma_start(tab_words[0][:], words_in_hbm(0))
+        nc.sync.dma_start(tab_words[1][:, 0:SPLIT], words_in_hbm(1)[:, 0:SPLIT])
+        nc.sync.dma_start(w_raw[0][:], w_in_hbm(0))
+        nc.sync.dma_start(tab_words[1][:, SPLIT:T], words_in_hbm(1)[:, SPLIT:T])
+        nc.sync.dma_start(w_raw[1][:], w_in_hbm(1))
+
+        nc.vector.memset(tab_scales[32:64, :].bitcast(I32), 0)
+        nc.vector.memset(tab_scales[64:128, :].bitcast(I32), 0)
+        for a in range(PASSES):
+            nc.vector.memset(planes[a][:].bitcast(I32), 0)
+
+        nc.vector.tensor_copy(picked_scales[:], tab_scales[:].indirect(offsets[:]))
+        moves = [(a, q) for a in range(PASSES) for q in range(4)]
+        for n, (a, q) in enumerate(moves):
+            queue = nc.scalar if n < HW_MOVES else nc.gpsimd
+            src = BLOCKS * a + 4 * q
+            dst = 32 * q
+            queue.dma_start(planes[a][dst : dst + 4, :].bitcast(I32), picked_scales[src : src + 4, :].bitcast(I32))
+
+        def gather(a, lo, hi, tag):
+            t = keep.tile([P, hi - lo], U32, name=f"picked{a}_{lo}", tag=tag, align_bytes=64)
+            nc.vector.tensor_copy(t[:], tab_words[a][:].bitcast(U32).indirect(offsets[:, lo // PER_COL : hi // PER_COL]))
+            return t
+
+        def round_w(a, tag):
+            t = keep.tile([P, M, PACK], BF16, name=f"w_bf{a}", tag=tag, align_bytes=64)
+            dst = t[:].rearrange("p (c e) i -> p c i e", e=4)
+            src = w_raw[a][:].rearrange("p i (c e) -> p c i e", e=4)
+            if a == 0:
+                nc.vector.tensor_copy(dst, src)
+            else:
+                nc.scalar.copy(dst, src)
+            return t
+
+        def quantise_w(a, t):
+            nc.vector.quantize_mx(
+                out=w_codes[a][:].bitcast(FP8X4), scales=w_scales[a][:], in_=t[:].rearrange("p n i -> p (n i)")
+            )
+
+        acc = [psum.tile([P, M], F32, name=f"acc{j}") for j in range(S // P)]
+
+        def multiply(a, g, picked, lo):
+            for j in range(S // P):
+                c = g * S + j * P
+                nc.tensor.matmul_mx(
+                    out=acc[j][:],
+                    lhsT=picked[:, c - lo : c - lo + P].bitcast(FP8X4),
+                    lhsT_scale=planes[a][:, c : c + P],
+                    rhs=w_codes[a][:].bitcast(FP8X4),
+                    rhs_scale=w_scales[a][:],
+                    start=(a == 0 and g == 0),
+                    stop=(a == PASSES - 1 and g == G - 1),
+                )
+
+        first = gather(0, 0, N_LIST, "first")
+        quantise_w(0, round_w(0, "w_bf0"))
+        for g in range(G):
+            multiply(0, g, first, 0)
+        second = gather(1, 0, 2 * S, "second")
+        quantise_w(1, round_w(1, "handover"))
+        for g in range(G - 1):
+            multiply(1, g, second, 0)
+        last = gather(1, 2 * S, N_LIST, "handover")
+        multiply(1, G - 1, last, 2 * S)
+
+        for j in range(S // P):
+            res = keep.tile([P, M], F32, name=f"res{j}")
+            if j % 2 == 0:
+                nc.scalar.copy(res[:], acc[j][:])
+            else:
+                nc.vector.tensor_copy(res[:], acc[j][:])
+            nc.sync.dma_start(out[j * P : (j + 1) * P, :], res[:])

@@ -22,7 +22,6 @@ PER_COL = 16
 WORD_BYTES = K_PASS * T
 BLOCKS = K_PASS // 32
 SPLIT = T // 2
-HW_MOVES = 6
 
 
 def tile_list_tabbag_tm_none_kernel(tc, tab, w, offs, out):
@@ -38,7 +37,7 @@ def tile_list_tabbag_tm_none_kernel(tc, tab, w, offs, out):
         w_codes = [keep.tile([P, M], U32, name=f"w_codes{a}", align_bytes=64) for a in range(PASSES)]
         w_scales = [keep.tile([P, M], U8, name=f"w_scales{a}", align_bytes=64) for a in range(PASSES)]
         picked_scales = keep.tile([P, N_LIST], U8, name="picked_scales", align_bytes=64)
-        planes = [keep.tile([P, N_LIST], U8, name=f"planes{a}", align_bytes=64) for a in range(PASSES)]
+        planes = keep.tile([P, PASSES, N_LIST], U8, name="planes", align_bytes=64)
 
         def words_in_hbm(a):
             return tab[a, 0:WORD_BYTES].rearrange("(p b) -> p b", p=P).bitcast(I32)
@@ -47,29 +46,26 @@ def tile_list_tabbag_tm_none_kernel(tc, tab, w, offs, out):
             return w[a * K_PASS : (a + 1) * K_PASS, :].rearrange("(p i) n -> p i n", i=PACK)
 
         nc.sync.dma_start(offsets[:], offs)
-        for a in range(PASSES):
-            nc.sync.dma_start(
-                tab_scales[BLOCKS * a : BLOCKS * (a + 1), :].bitcast(I32),
-                tab[a, WORD_BYTES : WORD_BYTES + BLOCKS * T].rearrange("(q t) -> q t", q=BLOCKS).bitcast(I32),
-            )
         nc.sync.dma_start(tab_words[0][:], words_in_hbm(0))
         nc.sync.dma_start(tab_words[1][:, 0:SPLIT], words_in_hbm(1)[:, 0:SPLIT])
         nc.sync.dma_start(w_raw[0][:], w_in_hbm(0))
         nc.sync.dma_start(tab_words[1][:, SPLIT:T], words_in_hbm(1)[:, SPLIT:T])
         nc.sync.dma_start(w_raw[1][:], w_in_hbm(1))
 
-        nc.vector.memset(tab_scales[32:64, :].bitcast(I32), 0)
-        nc.vector.memset(tab_scales[64:128, :].bitcast(I32), 0)
+        nc.vector.memset(tab_scales[:].bitcast(I32), 0)
+        nc.vector.memset(planes[:].rearrange("p a n -> p (a n)").bitcast(I32), 0)
         for a in range(PASSES):
-            nc.vector.memset(planes[a][:].bitcast(I32), 0)
+            nc.scalar.dma_start(
+                tab_scales[4 * a : P : 8, :].bitcast(I32),
+                tab[a, WORD_BYTES : WORD_BYTES + BLOCKS * T].rearrange("(q t) -> q t", q=BLOCKS).bitcast(I32),
+            )
 
         nc.vector.tensor_copy(picked_scales[:], tab_scales[:].indirect(offsets[:]))
-        moves = [(a, q) for a in range(PASSES) for q in range(4)]
-        for n, (a, q) in enumerate(moves):
-            queue = nc.scalar if n < HW_MOVES else nc.gpsimd
-            src = BLOCKS * a + 4 * q
-            dst = 32 * q
-            queue.dma_start(planes[a][dst : dst + 4, :].bitcast(I32), picked_scales[src : src + 4, :].bitcast(I32))
+        for q in range(4):
+            nc.scalar.dma_start(
+                planes[32 * q : 32 * q + 4, :, :].bitcast(I32),
+                picked_scales[32 * q : 32 * q + 32 : 4, :].bitcast(I32),
+            )
 
         def gather(a, lo, hi, tag):
             t = keep.tile([P, hi - lo], U32, name=f"picked{a}_{lo}", tag=tag, align_bytes=64)
@@ -99,7 +95,7 @@ def tile_list_tabbag_tm_none_kernel(tc, tab, w, offs, out):
                 nc.tensor.matmul_mx(
                     out=acc[j][:],
                     lhsT=picked[:, c - lo : c - lo + P].bitcast(FP8X4),
-                    lhsT_scale=planes[a][:, c : c + P],
+                    lhsT_scale=planes[:, a, c : c + P],
                     rhs=w_codes[a][:].bitcast(FP8X4),
                     rhs_scale=w_scales[a][:],
                     start=(a == 0 and g == 0),

@@ -21,7 +21,7 @@ N_LIST = G * S
 PER_COL = 16
 WORD_BYTES = K_PASS * T
 BLOCKS = K_PASS // 32
-SPLIT = T // 2
+SPLIT = 3 * T // 4
 
 
 def tile_list_tabbag_tm_none_kernel(tc, tab, w, offs, out):
@@ -31,13 +31,13 @@ def tile_list_tabbag_tm_none_kernel(tc, tab, w, offs, out):
         psum = ctx.enter_context(tc.psum_pool(name="psum", bufs=1))
 
         offsets = keep.tile([P, N_LIST // PER_COL], U16, name="offsets")
-        tab_scales = keep.tile([P, T], U8, name="tab_scales", align_bytes=64)
-        tab_words = [keep.tile([P, T], I32, name=f"tab_words{a}", align_bytes=64) for a in range(PASSES)]
-        w_raw = [keep.tile([P, PACK, M], F32, name=f"w_raw{a}", align_bytes=64) for a in range(PASSES)]
+        tab_scales = keep.tile([P, T], U8, name="tab_scales", tag="second_window", align_bytes=64)
+        tab_words = [keep.tile([P, T], I32, name="tab_words0", align_bytes=64)]
+        w_raw = []
         w_codes = [keep.tile([P, M], U32, name=f"w_codes{a}", align_bytes=64) for a in range(PASSES)]
         w_scales = [keep.tile([P, M], U8, name=f"w_scales{a}", align_bytes=64) for a in range(PASSES)]
         picked_scales = keep.tile([P, N_LIST], U8, name="picked_scales", align_bytes=64)
-        planes = keep.tile([P, PASSES, N_LIST], U8, name="planes", align_bytes=64)
+        planes = []
 
         def words_in_hbm(a):
             return tab[a, 0:WORD_BYTES].rearrange("(p b) -> p b", p=P).bitcast(I32)
@@ -46,26 +46,35 @@ def tile_list_tabbag_tm_none_kernel(tc, tab, w, offs, out):
             return w[a * K_PASS : (a + 1) * K_PASS, :].rearrange("(p i) n -> p i n", i=PACK)
 
         nc.sync.dma_start(offsets[:], offs)
-        nc.sync.dma_start(tab_words[0][:], words_in_hbm(0))
-        nc.sync.dma_start(tab_words[1][:, 0:SPLIT], words_in_hbm(1)[:, 0:SPLIT])
-        nc.sync.dma_start(w_raw[0][:], w_in_hbm(0))
-        nc.sync.dma_start(tab_words[1][:, SPLIT:T], words_in_hbm(1)[:, SPLIT:T])
-        nc.sync.dma_start(w_raw[1][:], w_in_hbm(1))
-
-        nc.vector.memset(tab_scales[:].bitcast(I32), 0)
-        nc.vector.memset(planes[:].rearrange("p a n -> p (a n)").bitcast(I32), 0)
         for a in range(PASSES):
-            nc.scalar.dma_start(
-                tab_scales[4 * a : P : 8, :].bitcast(I32),
+            nc.sync.dma_start(
+                tab_scales[96 + a : P : 2, :].bitcast(I32),
                 tab[a, WORD_BYTES : WORD_BYTES + BLOCKS * T].rearrange("(q t) -> q t", q=BLOCKS).bitcast(I32),
             )
+        nc.sync.dma_start(tab_words[0][:], words_in_hbm(0))
+
+        def load_w(a):
+            w_raw.append(keep.tile([P, PACK, M], F32, name=f"w_raw{a}", tag="w_raw", align_bytes=64))
+            nc.sync.dma_start(w_raw[a][:], w_in_hbm(a))
+
+        load_w(0)
+
+        nc.vector.memset(tab_scales[0:96, :].bitcast(I32), 0)
 
         nc.vector.tensor_copy(picked_scales[:], tab_scales[:].indirect(offsets[:]))
-        for q in range(4):
-            nc.scalar.dma_start(
-                planes[32 * q : 32 * q + 4, :, :].bitcast(I32),
-                picked_scales[32 * q : 32 * q + 32 : 4, :].bitcast(I32),
-            )
+
+        def move_scales(a, tag):
+            planes.append(keep.tile([P, N_LIST], U8, name=f"planes{a}", tag=tag, align_bytes=64))
+            nc.vector.memset(planes[a][:].bitcast(I32), 0)
+            for r in range(4):
+                nc.sync.dma_start(
+                    planes[a][r:P:32, :].bitcast(I32), picked_scales[96 + 2 * r + a : P : 8, :].bitcast(I32)
+                )
+
+        tab_words.append(keep.tile([P, T], I32, name="tab_words1", tag="second_window", align_bytes=64))
+        nc.sync.dma_start(tab_words[1][:, 0:SPLIT], words_in_hbm(1)[:, 0:SPLIT])
+        move_scales(0, "planes0")
+        nc.sync.dma_start(tab_words[1][:, SPLIT:T], words_in_hbm(1)[:, SPLIT:T])
 
         def gather(a, lo, hi, tag):
             t = keep.tile([P, hi - lo], U32, name=f"picked{a}_{lo}", tag=tag, align_bytes=64)
@@ -76,10 +85,7 @@ def tile_list_tabbag_tm_none_kernel(tc, tab, w, offs, out):
             t = keep.tile([P, M, PACK], BF16, name=f"w_bf{a}", tag=tag, align_bytes=64)
             dst = t[:].rearrange("p (c e) i -> p c i e", e=4)
             src = w_raw[a][:].rearrange("p i (c e) -> p c i e", e=4)
-            if a == 0:
-                nc.vector.tensor_copy(dst, src)
-            else:
-                nc.scalar.copy(dst, src)
+            nc.scalar.copy(dst, src)
             return t
 
         def quantise_w(a, t):
@@ -95,7 +101,7 @@ def tile_list_tabbag_tm_none_kernel(tc, tab, w, offs, out):
                 nc.tensor.matmul_mx(
                     out=acc[j][:],
                     lhsT=picked[:, c - lo : c - lo + P].bitcast(FP8X4),
-                    lhsT_scale=planes[:, a, c : c + P],
+                    lhsT_scale=planes[a][:, c : c + P],
                     rhs=w_codes[a][:].bitcast(FP8X4),
                     rhs_scale=w_scales[a][:],
                     start=(a == 0 and g == 0),
@@ -103,7 +109,9 @@ def tile_list_tabbag_tm_none_kernel(tc, tab, w, offs, out):
                 )
 
         first = gather(0, 0, N_LIST, "first")
-        quantise_w(0, round_w(0, "w_bf0"))
+        quantise_w(0, round_w(0, "late_plane"))
+        load_w(1)
+        move_scales(1, "late_plane")
         for g in range(G):
             multiply(0, g, first, 0)
         second = gather(1, 0, 2 * S, "second")

@@ -21,7 +21,8 @@ N_LIST = G * S
 PER_COL = 16
 WORD_BYTES = K_PASS * T
 BLOCKS = K_PASS // 32
-SPLIT = 3 * T // 4
+HALF = M // 2
+ROW0 = P - PASSES * BLOCKS
 
 
 def tile_list_tabbag_tm_none_kernel(tc, tab, w, offs, out):
@@ -31,8 +32,8 @@ def tile_list_tabbag_tm_none_kernel(tc, tab, w, offs, out):
         psum = ctx.enter_context(tc.psum_pool(name="psum", bufs=1))
 
         offsets = keep.tile([P, N_LIST // PER_COL], U16, name="offsets")
-        tab_scales = keep.tile([P, T], U8, name="tab_scales", tag="second_window", align_bytes=64)
-        tab_words = [keep.tile([P, T], I32, name="tab_words0", align_bytes=64)]
+        tab_scales = keep.tile([P, T], U8, name="tab_scales", align_bytes=64)
+        tab_words = [keep.tile([P, T], I32, name=f"tab_words{a}", align_bytes=64) for a in range(PASSES)]
         w_raw = []
         w_codes = [keep.tile([P, M], U32, name=f"w_codes{a}", align_bytes=64) for a in range(PASSES)]
         w_scales = [keep.tile([P, M], U8, name=f"w_scales{a}", align_bytes=64) for a in range(PASSES)]
@@ -46,20 +47,20 @@ def tile_list_tabbag_tm_none_kernel(tc, tab, w, offs, out):
             return w[a * K_PASS : (a + 1) * K_PASS, :].rearrange("(p i) n -> p i n", i=PACK)
 
         nc.sync.dma_start(offsets[:], offs)
-        for a in range(PASSES):
-            nc.sync.dma_start(
-                tab_scales[96 + a : P : 2, :].bitcast(I32),
-                tab[a, WORD_BYTES : WORD_BYTES + BLOCKS * T].rearrange("(q t) -> q t", q=BLOCKS).bitcast(I32),
-            )
-        nc.sync.dma_start(tab_words[0][:], words_in_hbm(0))
+        nc.sync.dma_start(
+            tab_scales[ROW0:P, :].bitcast(I32),
+            tab[:, WORD_BYTES : WORD_BYTES + BLOCKS * T].rearrange("a (q t) -> q a t", q=BLOCKS).bitcast(I32),
+        )
 
         def load_w(a):
             w_raw.append(keep.tile([P, PACK, M], F32, name=f"w_raw{a}", tag="w_raw", align_bytes=64))
             nc.sync.dma_start(w_raw[a][:], w_in_hbm(a))
 
+        nc.sync.dma_start(tab_words[0][:], words_in_hbm(0))
         load_w(0)
+        nc.sync.dma_start(tab_words[1][:], words_in_hbm(1))
 
-        nc.vector.memset(tab_scales[0:96, :].bitcast(I32), 0)
+        nc.vector.memset(tab_scales[0:ROW0, :].bitcast(I32), 0)
 
         nc.vector.tensor_copy(picked_scales[:], tab_scales[:].indirect(offsets[:]))
 
@@ -68,63 +69,71 @@ def tile_list_tabbag_tm_none_kernel(tc, tab, w, offs, out):
             nc.vector.memset(planes[a][:].bitcast(I32), 0)
             for r in range(4):
                 nc.sync.dma_start(
-                    planes[a][r:P:32, :].bitcast(I32), picked_scales[96 + 2 * r + a : P : 8, :].bitcast(I32)
+                    planes[a][r:P:32, :].bitcast(I32), picked_scales[ROW0 + 2 * r + a : P : 8, :].bitcast(I32)
                 )
 
-        tab_words.append(keep.tile([P, T], I32, name="tab_words1", tag="second_window", align_bytes=64))
-        nc.sync.dma_start(tab_words[1][:, 0:SPLIT], words_in_hbm(1)[:, 0:SPLIT])
         move_scales(0, "planes0")
-        nc.sync.dma_start(tab_words[1][:, SPLIT:T], words_in_hbm(1)[:, SPLIT:T])
 
         def gather(a, lo, hi, tag):
             t = keep.tile([P, hi - lo], U32, name=f"picked{a}_{lo}", tag=tag, align_bytes=64)
             nc.vector.tensor_copy(t[:], tab_words[a][:].bitcast(U32).indirect(offsets[:, lo // PER_COL : hi // PER_COL]))
             return t
 
-        def round_w(a, tag):
-            t = keep.tile([P, M, PACK], BF16, name=f"w_bf{a}", tag=tag, align_bytes=64)
+        def round_w(a, lo, hi, tag):
+            t = keep.tile([P, hi - lo, PACK], BF16, name=f"w_bf{a}_{lo}", tag=tag, align_bytes=64)
             dst = t[:].rearrange("p (c e) i -> p c i e", e=4)
-            src = w_raw[a][:].rearrange("p i (c e) -> p c i e", e=4)
+            src = w_raw[a][:, :, lo:hi].rearrange("p i (c e) -> p c i e", e=4)
             nc.scalar.copy(dst, src)
             return t
 
-        def quantise_w(a, t):
+        def quantise_w(a, lo, hi, t):
             nc.vector.quantize_mx(
-                out=w_codes[a][:].bitcast(FP8X4), scales=w_scales[a][:], in_=t[:].rearrange("p n i -> p (n i)")
+                out=w_codes[a][:, lo:hi].bitcast(FP8X4),
+                scales=w_scales[a][:, lo:hi],
+                in_=t[:].rearrange("p n i -> p (n i)"),
             )
 
-        acc = [psum.tile([P, M], F32, name=f"acc{j}") for j in range(S // P)]
+        parts = [(0, 0, HALF), (0, HALF, M)] + [(j, 0, M) for j in range(1, S // P)]
+        acc = [psum.tile([P, n1 - n0], F32, name=f"acc{j}_{n0}") for j, n0, n1 in parts]
 
-        def multiply(a, g, picked, lo):
-            for j in range(S // P):
+        def multiply(a, g, picked, lo, blocks=range(S // P)):
+            for (j, n0, n1), bank in zip(parts, acc):
+                if j not in blocks:
+                    continue
                 c = g * S + j * P
                 nc.tensor.matmul_mx(
-                    out=acc[j][:],
+                    out=bank[:],
                     lhsT=picked[:, c - lo : c - lo + P].bitcast(FP8X4),
                     lhsT_scale=planes[a][:, c : c + P],
-                    rhs=w_codes[a][:].bitcast(FP8X4),
-                    rhs_scale=w_scales[a][:],
+                    rhs=w_codes[a][:, n0:n1].bitcast(FP8X4),
+                    rhs_scale=w_scales[a][:, n0:n1],
                     start=(a == 0 and g == 0),
                     stop=(a == PASSES - 1 and g == G - 1),
                 )
 
         first = gather(0, 0, N_LIST, "first")
-        quantise_w(0, round_w(0, "late_plane"))
+        quantise_w(0, 0, M, round_w(0, 0, M, "late_plane"))
         load_w(1)
         move_scales(1, "late_plane")
         for g in range(G):
             multiply(0, g, first, 0)
         second = gather(1, 0, 2 * S, "second")
-        quantise_w(1, round_w(1, "handover"))
-        for g in range(G - 1):
-            multiply(1, g, second, 0)
-        last = gather(1, 2 * S, N_LIST, "handover")
-        multiply(1, G - 1, last, 2 * S)
+        quantise_w(1, 0, HALF, round_w(1, 0, HALF, "w_bf1_lo"))
+        quantise_w(1, HALF, M, round_w(1, HALF, M, "w_bf1_hi"))
+        last = gather(1, 2 * S, N_LIST, "w_raw")
+        early, late = range(0, 2), range(2, S // P)
+        multiply(1, 0, second, 0)
+        multiply(1, 1, second, 0, early)
+        multiply(1, 2, last, 2 * S, early)
+        for j in late:
+            multiply(1, 1, second, 0, [j])
+            multiply(1, 2, last, 2 * S, [j])
 
-        for j in range(S // P):
-            res = keep.tile([P, M], F32, name=f"res{j}")
-            if j % 2 == 0:
-                nc.scalar.copy(res[:], acc[j][:])
+        res = [keep.tile([P, M], F32, name=f"res{j}") for j in range(S // P)]
+        for i, ((j, n0, n1), bank) in enumerate(zip(parts, acc)):
+            if i % 2 == 0:
+                nc.scalar.copy(res[j][:, n0:n1], bank[:])
             else:
-                nc.vector.tensor_copy(res[:], acc[j][:])
-            nc.sync.dma_start(out[j * P : (j + 1) * P, :], res[:])
+                nc.vector.tensor_copy(res[j][:, n0:n1], bank[:])
+            if n1 == M:
+                nc.sync.dma_start(out[j * P : (j + 1) * P, :], res[j][:])

@@ -29,16 +29,17 @@ def tile_list_tabbag_tm_none_kernel(tc, tab, w, offs, out):
     nc = tc.nc
     with ExitStack() as ctx:
         keep = ctx.enter_context(tc.tile_pool(name="keep", bufs=1))
+        ring = ctx.enter_context(tc.tile_pool(name="ring", bufs=1))
         psum = ctx.enter_context(tc.psum_pool(name="psum", bufs=1))
 
         offsets = keep.tile([P, N_LIST // PER_COL], U16, name="offsets")
         tab_scales = keep.tile([P, T], U8, name="tab_scales", align_bytes=64)
         tab_words = [keep.tile([P, T], I32, name=f"tab_words{a}", align_bytes=64) for a in range(PASSES)]
-        w_raw = []
+        w_raw = {}
         w_codes = [keep.tile([P, M], U32, name=f"w_codes{a}", align_bytes=64) for a in range(PASSES)]
         w_scales = [keep.tile([P, M], U8, name=f"w_scales{a}", align_bytes=64) for a in range(PASSES)]
         picked_scales = keep.tile([P, N_LIST], U8, name="picked_scales", align_bytes=64)
-        planes = []
+        planes = {}
 
         def words_in_hbm(a):
             return tab[a, 0:WORD_BYTES].rearrange("(p b) -> p b", p=P).bitcast(I32)
@@ -46,51 +47,56 @@ def tile_list_tabbag_tm_none_kernel(tc, tab, w, offs, out):
         def w_in_hbm(a):
             return w[a * K_PASS : (a + 1) * K_PASS, :].rearrange("(p i) n -> p i n", i=PACK)
 
-        nc.sync.dma_start(offsets[:], offs)
         nc.sync.dma_start(
             tab_scales[ROW0:P, :].bitcast(I32),
             tab[:, WORD_BYTES : WORD_BYTES + BLOCKS * T].rearrange("a (q t) -> q a t", q=BLOCKS).bitcast(I32),
         )
+        nc.sync.dma_start(offsets[:], offs)
 
-        def load_w(a):
-            w_raw.append(keep.tile([P, PACK, M], F32, name=f"w_raw{a}", tag="w_raw", align_bytes=64))
-            nc.sync.dma_start(w_raw[a][:], w_in_hbm(a))
+        def load_w(a, n0, n1):
+            w_raw[a, n0] = ring.tile([P, PACK, n1 - n0], F32, name=f"w_raw{a}_{n0}", offset=n0 * PACK * 4, align_bytes=64)
+            nc.sync.dma_start(w_raw[a, n0][:], w_in_hbm(a)[:, :, n0:n1])
 
         nc.sync.dma_start(tab_words[0][:], words_in_hbm(0))
-        load_w(0)
+        load_w(0, 0, M)
         nc.sync.dma_start(tab_words[1][:], words_in_hbm(1))
 
         nc.vector.memset(tab_scales[0:ROW0, :].bitcast(I32), 0)
 
         nc.vector.tensor_copy(picked_scales[:], tab_scales[:].indirect(offsets[:]))
 
-        def move_scales(a, tag):
-            planes.append(keep.tile([P, N_LIST], U8, name=f"planes{a}", tag=tag, align_bytes=64))
-            nc.vector.memset(planes[a][:].bitcast(I32), 0)
-            for r in range(4):
-                nc.sync.dma_start(
-                    planes[a][r:P:32, :].bitcast(I32), picked_scales[ROW0 + 2 * r + a : P : 8, :].bitcast(I32)
-                )
+        def move_scales(ranges, tag):
+            plane = keep.tile([P, sum(hi - lo for a, lo, hi in ranges)], U8, name=tag + "_plane", tag=tag, align_bytes=64)
+            nc.vector.memset(plane[:].bitcast(I32), 0)
+            at = 0
+            for a, lo, hi in ranges:
+                for r in range(4):
+                    nc.sync.dma_start(
+                        plane[r:P:32, at : at + hi - lo].bitcast(I32),
+                        picked_scales[ROW0 + 2 * r + a : P : 8, lo:hi].bitcast(I32),
+                    )
+                for c in range(lo, hi, P):
+                    planes[a, c] = plane[:, at + c - lo : at + c - lo + P]
+                at = at + hi - lo
 
-        move_scales(0, "planes0")
+        move_scales([(0, 0, N_LIST // 2)], "early")
 
-        def gather(a, lo, hi, tag):
-            t = keep.tile([P, hi - lo], U32, name=f"picked{a}_{lo}", tag=tag, align_bytes=64)
+        def gather(a, lo, hi, at):
+            t = ring.tile([P, hi - lo], U32, name=f"picked{a}_{lo}", offset=at, align_bytes=64)
             nc.vector.tensor_copy(t[:], tab_words[a][:].bitcast(U32).indirect(offsets[:, lo // PER_COL : hi // PER_COL]))
             return t
 
-        def round_w(a, lo, hi, tag):
-            t = keep.tile([P, hi - lo, PACK], BF16, name=f"w_bf{a}_{lo}", tag=tag, align_bytes=64)
-            dst = t[:].rearrange("p (c e) i -> p c i e", e=4)
-            src = w_raw[a][:, :, lo:hi].rearrange("p i (c e) -> p c i e", e=4)
-            nc.scalar.copy(dst, src)
+        def round_w(a, starts, tag):
+            t = keep.tile([P, M, PACK], BF16, name=f"w_bf{a}", tag=tag, align_bytes=64)
+            width = M // len(starts)
+            for n0 in starts:
+                dst = t[:, n0 : n0 + width, :].rearrange("p (c e) i -> p c i e", e=4)
+                nc.scalar.copy(dst, w_raw[a, n0][:].rearrange("p i (c e) -> p c i e", e=4))
             return t
 
-        def quantise_w(a, lo, hi, t):
+        def quantise_w(a, t):
             nc.vector.quantize_mx(
-                out=w_codes[a][:, lo:hi].bitcast(FP8X4),
-                scales=w_scales[a][:, lo:hi],
-                in_=t[:].rearrange("p n i -> p (n i)"),
+                out=w_codes[a][:].bitcast(FP8X4), scales=w_scales[a][:], in_=t[:].rearrange("p n i -> p (n i)")
             )
 
         parts = [(0, 0, HALF), (0, HALF, M)] + [(j, 0, M) for j in range(1, S // P)]
@@ -104,23 +110,23 @@ def tile_list_tabbag_tm_none_kernel(tc, tab, w, offs, out):
                 nc.tensor.matmul_mx(
                     out=bank[:],
                     lhsT=picked[:, c - lo : c - lo + P].bitcast(FP8X4),
-                    lhsT_scale=planes[a][:, c : c + P],
+                    lhsT_scale=planes[a, c],
                     rhs=w_codes[a][:, n0:n1].bitcast(FP8X4),
                     rhs_scale=w_scales[a][:, n0:n1],
                     start=(a == 0 and g == 0),
                     stop=(a == PASSES - 1 and g == G - 1),
                 )
 
-        first = gather(0, 0, N_LIST, "first")
-        quantise_w(0, 0, M, round_w(0, 0, M, "late_plane"))
-        load_w(1)
-        move_scales(1, "late_plane")
+        first = gather(0, 0, N_LIST, 4096)
+        quantise_w(0, round_w(0, [0], "late_plane"))
+        load_w(1, 0, HALF)
+        load_w(1, HALF, M)
+        move_scales([(0, N_LIST // 2, N_LIST), (1, 0, N_LIST)], "late_plane")
         for g in range(G):
             multiply(0, g, first, 0)
-        second = gather(1, 0, 2 * S, "second")
-        quantise_w(1, 0, HALF, round_w(1, 0, HALF, "w_bf1_lo"))
-        quantise_w(1, HALF, M, round_w(1, HALF, M, "w_bf1_hi"))
-        last = gather(1, 2 * S, N_LIST, "w_raw")
+        second = gather(1, 0, 2 * S, 4096 + 4 * N_LIST)
+        quantise_w(1, round_w(1, [0, HALF], "w_bf1"))
+        last = gather(1, 2 * S, N_LIST, HALF * PACK * 4)
         early, late = range(0, 2), range(2, S // P)
         multiply(1, 0, second, 0)
         multiply(1, 1, second, 0, early)

@@ -65,13 +65,13 @@ def tile_list_tabbag_tm_none_kernel(tc, tab, w, offs, out):
 
         nc.vector.tensor_copy(picked_scales[:], tab_scales[:].indirect(offsets[:]))
 
-        def move_scales(ranges, tag):
+        def move_scales(ranges, tag, queue):
             plane = keep.tile([P, sum(hi - lo for a, lo, hi in ranges)], U8, name=tag + "_plane", tag=tag, align_bytes=64)
             nc.vector.memset(plane[:].bitcast(I32), 0)
             at = 0
             for a, lo, hi in ranges:
                 for r in range(4):
-                    nc.sync.dma_start(
+                    queue.dma_start(
                         plane[r:P:32, at : at + hi - lo].bitcast(I32),
                         picked_scales[ROW0 + 2 * r + a : P : 8, lo:hi].bitcast(I32),
                     )
@@ -79,7 +79,7 @@ def tile_list_tabbag_tm_none_kernel(tc, tab, w, offs, out):
                     planes[a, c] = plane[:, at + c - lo : at + c - lo + P]
                 at = at + hi - lo
 
-        move_scales([(0, 0, N_LIST // 2)], "early")
+        move_scales([(0, 0, N_LIST // 2)], "early", nc.scalar)
 
         def gather(a, lo, hi, at):
             t = ring.tile([P, hi - lo], U32, name=f"picked{a}_{lo}", offset=at, align_bytes=64)
@@ -121,7 +121,7 @@ def tile_list_tabbag_tm_none_kernel(tc, tab, w, offs, out):
         quantise_w(0, round_w(0, [0], "late_plane"))
         load_w(1, 0, HALF)
         load_w(1, HALF, M)
-        move_scales([(0, N_LIST // 2, N_LIST), (1, 0, N_LIST)], "late_plane")
+        move_scales([(0, N_LIST // 2, N_LIST), (1, 0, N_LIST)], "late_plane", nc.sync)
         for g in range(G):
             multiply(0, g, first, 0)
         second = gather(1, 0, 2 * S, 4096 + 4 * N_LIST)

@@ -23,6 +23,10 @@ WORD_BYTES = K_PASS * T
 BLOCKS = K_PASS // 32
 HALF = M // 2
 ROW0 = P - PASSES * BLOCKS
+EARLY = 768
+CUT1, CUT2, LAST = 640, 1152, N_LIST - S
+SPLIT = [1,3]
+COL_RAW, COL_BF = PACK * 4, PACK * 2
 
 
 def tile_list_tabbag_tm_none_kernel(tc, tab, w, offs, out):
@@ -32,114 +36,145 @@ def tile_list_tabbag_tm_none_kernel(tc, tab, w, offs, out):
         ring = ctx.enter_context(tc.tile_pool(name="ring", bufs=1))
         psum = ctx.enter_context(tc.psum_pool(name="psum", bufs=1))
 
+        at_scales = 0
+        at_raw0b = 2 * T
+        at_bf0a = 3 * T
+
         offsets = keep.tile([P, N_LIST // PER_COL], U16, name="offsets")
-        tab_scales = keep.tile([P, T], U8, name="tab_scales", align_bytes=64)
+        tab_scales = ring.tile([P, T], U8, name="tab_scales", offset=at_scales, align_bytes=64)
         tab_words = [keep.tile([P, T], I32, name=f"tab_words{a}", align_bytes=64) for a in range(PASSES)]
-        w_raw = {}
         w_codes = [keep.tile([P, M], U32, name=f"w_codes{a}", align_bytes=64) for a in range(PASSES)]
         w_scales = [keep.tile([P, M], U8, name=f"w_scales{a}", align_bytes=64) for a in range(PASSES)]
         picked_scales = keep.tile([P, N_LIST], U8, name="picked_scales", align_bytes=64)
         planes = {}
+        picked = {}
 
-        def words_in_hbm(a):
-            return tab[a, 0:WORD_BYTES].rearrange("(p b) -> p b", p=P).bitcast(I32)
+        def load_words(a):
+            nc.sync.dma_start(tab_words[a][:], tab[a, 0:WORD_BYTES].rearrange("(p b) -> p b", p=P).bitcast(I32))
 
-        def w_in_hbm(a):
-            return w[a * K_PASS : (a + 1) * K_PASS, :].rearrange("(p i) n -> p i n", i=PACK)
+        def load_w(a, n0, raw):
+            rows = w[a * K_PASS : (a + 1) * K_PASS, :].rearrange("(p i) n -> p i n", i=PACK)
+            nc.sync.dma_start(raw[:], rows[:, :, n0 : n0 + raw.shape[2]])
 
+        def round_w(raw, dst):
+            nc.scalar.copy(
+                dst.rearrange("p (c e) i -> p c i e", e=4), raw[:].rearrange("p i (c e) -> p c i e", e=4)
+            )
+
+        def quantise_w(a, n0, n1, src):
+            nc.vector.quantize_mx(
+                out=w_codes[a][:, n0:n1].bitcast(FP8X4),
+                scales=w_scales[a][:, n0:n1],
+                in_=src.rearrange("p n i -> p (n i)"),
+            )
+
+        def move_scales(plane, at, a, lo, hi, k):
+            for r in range(4):
+                nc.sync.dma_start(
+                    plane[k + r : P : 32, at : at + hi - lo].bitcast(I32),
+                    picked_scales[ROW0 + 2 * r + a : P : 8, lo:hi].bitcast(I32),
+                )
+            for c in range(lo, hi, P):
+                planes[a, c] = plane[k:P, at + c - lo : at + c - lo + P]
+
+        def gather(a, lo, hi, t):
+            nc.vector.tensor_copy(t[:], tab_words[a][:].bitcast(U32).indirect(offsets[:, lo // PER_COL : hi // PER_COL]))
+            for c in range(lo, hi, P):
+                picked.setdefault((a, c), t[:, c - lo : c - lo + P])
+
+        raw0a = keep.tile([P, PACK, HALF], F32, name="raw0a", align_bytes=64)
+        raw0b = ring.tile([P, PACK, HALF], F32, name="raw0b", offset=at_raw0b, align_bytes=64)
         nc.sync.dma_start(
             tab_scales[ROW0:P, :].bitcast(I32),
             tab[:, WORD_BYTES : WORD_BYTES + BLOCKS * T].rearrange("a (q t) -> q a t", q=BLOCKS).bitcast(I32),
         )
         nc.sync.dma_start(offsets[:], offs)
-
-        def load_w(a, n0, n1):
-            w_raw[a, n0] = ring.tile([P, PACK, n1 - n0], F32, name=f"w_raw{a}_{n0}", offset=n0 * PACK * 4, align_bytes=64)
-            nc.sync.dma_start(w_raw[a, n0][:], w_in_hbm(a)[:, :, n0:n1])
-
-        nc.sync.dma_start(tab_words[0][:], words_in_hbm(0))
-        load_w(0, 0, M)
-        nc.sync.dma_start(tab_words[1][:], words_in_hbm(1))
+        load_words(0)
+        load_w(0, 0, raw0a)
+        load_words(1)
+        load_w(0, HALF, raw0b)
 
         nc.vector.memset(tab_scales[0:ROW0, :].bitcast(I32), 0)
-
+        early_plane = keep.tile([P, EARLY], U8, name="early_plane", align_bytes=64)
+        nc.vector.memset(early_plane[:].bitcast(I32), 0)
         nc.vector.tensor_copy(picked_scales[:], tab_scales[:].indirect(offsets[:]))
+        move_scales(early_plane, 0, 0, 0, EARLY, 0)
 
-        def move_scales(ranges, tag, queue):
-            plane = keep.tile([P, sum(hi - lo for a, lo, hi in ranges)], U8, name=tag + "_plane", tag=tag, align_bytes=64)
-            nc.vector.memset(plane[:].bitcast(I32), 0)
-            at = 0
-            for a, lo, hi in ranges:
-                for r in range(4):
-                    queue.dma_start(
-                        plane[r:P:32, at : at + hi - lo].bitcast(I32),
-                        picked_scales[ROW0 + 2 * r + a : P : 8, lo:hi].bitcast(I32),
-                    )
-                for c in range(lo, hi, P):
-                    planes[a, c] = plane[:, at + c - lo : at + c - lo + P]
-                at = at + hi - lo
+        cuts = [0, HALF, M]
+        raw1 = []
+        for n0, n1 in zip(cuts, cuts[1:]):
+            raw = ring.tile([P, PACK, n1 - n0], F32, name=f"raw1_{n0}", offset=at_scales + n0 * COL_RAW, align_bytes=64)
+            load_w(1, n0, raw)
+            raw1.append((n0, n1, raw))
 
-        move_scales([(0, 0, N_LIST // 2)], "early", nc.scalar)
+        gather(0, 0, N_LIST, keep.tile([P, N_LIST], U32, name="picked0", align_bytes=64))
+        bf0a = ring.tile([P, HALF, PACK], BF16, name="bf0a", offset=at_bf0a, align_bytes=64)
+        round_w(raw0a, bf0a[:])
+        quantise_w(0, 0, HALF, bf0a[:])
+        late_plane = ring.tile([P, 2 * N_LIST - EARLY], U8, name="late_plane", offset=at_bf0a, align_bytes=64)
+        nc.vector.memset(late_plane[:].bitcast(I32), 0)
+        move_scales(late_plane, 0, 0, EARLY, N_LIST, 0)
+        move_scales(late_plane, N_LIST - EARLY, 1, 0, N_LIST, 0)
 
-        def gather(a, lo, hi, at):
-            t = ring.tile([P, hi - lo], U32, name=f"picked{a}_{lo}", offset=at, align_bytes=64)
-            nc.vector.tensor_copy(t[:], tab_words[a][:].bitcast(U32).indirect(offsets[:, lo // PER_COL : hi // PER_COL]))
-            return t
+        gather(1, 0, CUT1, keep.tile([P, CUT1], U32, name="picked1_first", align_bytes=64))
+        bf0b = keep.tile([P, HALF, PACK], BF16, name="bf0b", align_bytes=64)
+        round_w(raw0b, bf0b[:])
+        quantise_w(0, HALF, M, bf0b[:])
+        gather(1, CUT1, CUT2, ring.tile([P, CUT2 - CUT1], U32, name="picked1_middle", offset=at_raw0b, align_bytes=64))
+        bf1 = keep.tile([P, M, PACK], BF16, name="bf1", align_bytes=64)
+        for n0, n1, raw in raw1:
+            round_w(raw, bf1[:, n0:n1, :])
+        for n0, n1 in zip([0, HALF, M], [0, HALF, M][1:]):
+            quantise_w(1, n0, n1, bf1[:, n0:n1, :])
+        gather(1, LAST, N_LIST, ring.tile([P, S], U32, name="picked1_last", offset=at_scales + cuts[-2] * COL_RAW, align_bytes=64))
 
-        def round_w(a, starts, tag):
-            t = keep.tile([P, M, PACK], BF16, name=f"w_bf{a}", tag=tag, align_bytes=64)
-            width = M // len(starts)
-            for n0 in starts:
-                dst = t[:, n0 : n0 + width, :].rearrange("p (c e) i -> p c i e", e=4)
-                nc.scalar.copy(dst, w_raw[a, n0][:].rearrange("p i (c e) -> p c i e", e=4))
-            return t
+        banks = {}
+        for j in range(S // P):
+            if j in SPLIT:
+                for n0 in (0, HALF):
+                    banks[j, n0] = (psum.tile([P, HALF], F32, name=f"acc{j}_{n0}"), n0)
+            else:
+                banks[j, 0] = banks[j, HALF] = (psum.tile([P, M], F32, name=f"acc{j}"), 0)
 
-        def quantise_w(a, t):
-            nc.vector.quantize_mx(
-                out=w_codes[a][:].bitcast(FP8X4), scales=w_scales[a][:], in_=t[:].rearrange("p n i -> p (n i)")
+        def one_pass(a, g, j, n0, n1):
+            bank, first_col = banks[j, n0]
+            c = g * S + j * P
+            nc.tensor.matmul_mx(
+                out=bank[:, n0 - first_col : n1 - first_col],
+                lhsT=picked[a, c].bitcast(FP8X4),
+                lhsT_scale=planes[a, c],
+                rhs=w_codes[a][:, n0:n1].bitcast(FP8X4),
+                rhs_scale=w_scales[a][:, n0:n1],
+                start=(a == 0 and g == 0 and n0 == first_col),
+                stop=(a == PASSES - 1 and g == G - 1),
             )
 
-        parts = [(0, 0, HALF), (0, HALF, M)] + [(j, 0, M) for j in range(1, S // P)]
-        acc = [psum.tile([P, n1 - n0], F32, name=f"acc{j}_{n0}") for j, n0, n1 in parts]
-
-        def multiply(a, g, picked, lo, blocks=range(S // P)):
-            for (j, n0, n1), bank in zip(parts, acc):
-                if j not in blocks:
-                    continue
-                c = g * S + j * P
-                nc.tensor.matmul_mx(
-                    out=bank[:],
-                    lhsT=picked[:, c - lo : c - lo + P].bitcast(FP8X4),
-                    lhsT_scale=planes[a, c],
-                    rhs=w_codes[a][:, n0:n1].bitcast(FP8X4),
-                    rhs_scale=w_scales[a][:, n0:n1],
-                    start=(a == 0 and g == 0),
-                    stop=(a == PASSES - 1 and g == G - 1),
-                )
-
-        first = gather(0, 0, N_LIST, 4096)
-        quantise_w(0, round_w(0, [0], "late_plane"))
-        load_w(1, 0, HALF)
-        load_w(1, HALF, M)
-        move_scales([(0, N_LIST // 2, N_LIST), (1, 0, N_LIST)], "late_plane", nc.sync)
-        for g in range(G):
-            multiply(0, g, first, 0)
-        second = gather(1, 0, 2 * S, 4096 + 4 * N_LIST)
-        quantise_w(1, round_w(1, [0, HALF], "w_bf1"))
-        last = gather(1, 2 * S, N_LIST, HALF * PACK * 4)
-        early, late = range(0, 2), range(2, S // P)
-        multiply(1, 0, second, 0)
-        multiply(1, 1, second, 0, early)
-        multiply(1, 2, last, 2 * S, early)
-        for j in late:
-            multiply(1, 1, second, 0, [j])
-            multiply(1, 2, last, 2 * S, [j])
-
-        res = [keep.tile([P, M], F32, name=f"res{j}") for j in range(S // P)]
-        for i, ((j, n0, n1), bank) in enumerate(zip(parts, acc)):
-            if i % 2 == 0:
-                nc.scalar.copy(res[j][:, n0:n1], bank[:])
+        def multiply(a, g, j):
+            if j in SPLIT:
+                one_pass(a, g, j, 0, HALF)
+                one_pass(a, g, j, HALF, M)
             else:
-                nc.vector.tensor_copy(res[j][:, n0:n1], bank[:])
+                one_pass(a, g, j, 0, M)
+
+        in_halves = [(j, 0) for j in range(S // P)] + [(1, 1), (0, 1)]
+        for n0 in (0, HALF):
+            for j, g in in_halves:
+                one_pass(0, g, j, n0, n0 + HALF)
+        for g in range(G):
+            for j in range(S // P):
+                if (j, g) not in in_halves:
+                    multiply(0, g, j)
+        for j, g in [(0, 0), (0, 1), (0, 2), (1, 0), (1, 1), (2, 0), (2, 1), (1, 2), (2, 2), (3, 0), (3, 1), (3, 2)]:
+            multiply(1, g, j)
+
+        parts = []
+        for j in range(S // P):
+            parts.extend([(j, 0, HALF), (j, HALF, M)] if j in SPLIT else [(j, 0, M)])
+        res = [keep.tile([P, M], F32, name=f"res{j}") for j in range(S // P)]
+        for i, (j, n0, n1) in enumerate(parts):
+            if "svsvsv"[i] == "s":
+                nc.scalar.copy(res[j][:, n0:n1], banks[j, n0][0][:])
+            else:
+                nc.vector.tensor_copy(res[j][:, n0:n1], banks[j, n0][0][:])
             if n1 == M:
                 nc.sync.dma_start(out[j * P : (j + 1) * P, :], res[j][:])

@@ -156,6 +156,17 @@ def tile_list_tabbag_tm_none_kernel(tc, tab, w, offs, out):
             else:
                 one_pass(a, g, j, 0, M)
 
+        for i, width in enumerate((512, 64)):
+            spare = psum.tile([P, width], F32, name=f"spare{i}")
+            nc.tensor.matmul_mx(
+                out=spare[:],
+                lhsT=w_codes[0][:, 0:P].bitcast(FP8X4),
+                lhsT_scale=w_scales[0][:, 0:P],
+                rhs=tab_words[1][:, 0:width].bitcast(FP8X4),
+                rhs_scale=picked_scales[:, 0:width],
+                start=True,
+                stop=True,
+            )
         in_halves = [(j, 0) for j in range(S // P)] + [(1, 1), (0, 1)]
         for n0 in (0, HALF):
             for j, g in in_halves:

@@ -21,171 +21,198 @@ N_LIST = G * S
 PER_COL = 16
 WORD_BYTES = K_PASS * T
 BLOCKS = K_PASS // 32
+QUADRANT = 32
+LIVE_ROWS = 4
 HALF = M // 2
 ROW0 = P - PASSES * BLOCKS
-EARLY = 768
-CUT1, CUT2, LAST = 640, 1152, N_LIST - S
-SPLIT = [1,3]
-COL_RAW, COL_BF = PACK * 4, PACK * 2
+
+EARLY = N_LIST // 2
+FIRST_END = S + P
+MIDDLE_END = FIRST_END + S
+LAST_START = N_LIST - S
+TWO_BANKS = (1, 3)
+WARM_UP_WIDTHS = (512, 64)
+RAW_HALF_BYTES = PACK * HALF * 4
 
 
 def tile_list_tabbag_tm_none_kernel(tc, tab, w, offs, out):
     nc = tc.nc
     with ExitStack() as ctx:
         keep = ctx.enter_context(tc.tile_pool(name="keep", bufs=1))
-        ring = ctx.enter_context(tc.tile_pool(name="ring", bufs=1))
+        reused = ctx.enter_context(tc.tile_pool(name="reused", bufs=1))
         psum = ctx.enter_context(tc.psum_pool(name="psum", bufs=1))
 
-        at_scales = 0
-        at_raw0b = 2 * T
-        at_bf0a = 3 * T
+        at_scale_rows = 0
+        at_raw0_second = 2 * T
+        at_rounded0_first = 3 * T
 
         offsets = keep.tile([P, N_LIST // PER_COL], U16, name="offsets")
-        tab_scales = ring.tile([P, T], U8, name="tab_scales", offset=at_scales, align_bytes=64)
+        scale_rows = reused.tile([P, T], U8, name="scale_rows", offset=at_scale_rows, align_bytes=64)
         tab_words = [keep.tile([P, T], I32, name=f"tab_words{a}", align_bytes=64) for a in range(PASSES)]
         w_codes = [keep.tile([P, M], U32, name=f"w_codes{a}", align_bytes=64) for a in range(PASSES)]
-        w_scales = [keep.tile([P, M], U8, name=f"w_scales{a}", align_bytes=64) for a in range(PASSES)]
-        picked_scales = keep.tile([P, N_LIST], U8, name="picked_scales", align_bytes=64)
-        planes = {}
-        picked = {}
+        w_planes = [keep.tile([P, M], U8, name=f"w_planes{a}", align_bytes=64) for a in range(PASSES)]
+        picked_rows = keep.tile([P, N_LIST], U8, name="picked_rows", align_bytes=64)
+        picked_words = {}
+        picked_planes = {}
 
         def load_words(a):
             nc.sync.dma_start(tab_words[a][:], tab[a, 0:WORD_BYTES].rearrange("(p b) -> p b", p=P).bitcast(I32))
 
         def load_w(a, n0, raw):
-            rows = w[a * K_PASS : (a + 1) * K_PASS, :].rearrange("(p i) n -> p i n", i=PACK)
-            nc.sync.dma_start(raw[:], rows[:, :, n0 : n0 + raw.shape[2]])
+            rows = w[a * K_PASS : (a + 1) * K_PASS, :].rearrange("(p t) n -> p t n", t=PACK)
+            nc.sync.dma_start(raw[:], rows[:, :, n0 : n0 + HALF])
 
-        def round_w(raw, dst):
+        def round_w(raw, rounded):
             nc.scalar.copy(
-                dst.rearrange("p (c e) i -> p c i e", e=4), raw[:].rearrange("p i (c e) -> p c i e", e=4)
+                rounded.rearrange("p (c e) t -> p c t e", e=4), raw[:].rearrange("p t (c e) -> p c t e", e=4)
             )
 
-        def quantise_w(a, n0, n1, src):
+        def quantise_w(a, n0, rounded):
             nc.vector.quantize_mx(
-                out=w_codes[a][:, n0:n1].bitcast(FP8X4),
-                scales=w_scales[a][:, n0:n1],
-                in_=src.rearrange("p n i -> p (n i)"),
+                out=w_codes[a][:, n0 : n0 + HALF].bitcast(FP8X4),
+                scales=w_planes[a][:, n0 : n0 + HALF],
+                in_=rounded.rearrange("p n t -> p (n t)"),
             )
 
-        def move_scales(plane, at, a, lo, hi, k):
-            for r in range(4):
+        def move_to_plane(plane, at, a, lo, hi):
+            for r in range(LIVE_ROWS):
                 nc.sync.dma_start(
-                    plane[k + r : P : 32, at : at + hi - lo].bitcast(I32),
-                    picked_scales[ROW0 + 2 * r + a : P : 8, lo:hi].bitcast(I32),
+                    plane[r:P:QUADRANT, at : at + hi - lo].bitcast(I32),
+                    picked_rows[ROW0 + PASSES * r + a : P : PASSES * LIVE_ROWS, lo:hi].bitcast(I32),
                 )
-            for c in range(lo, hi, P):
-                planes[a, c] = plane[k:P, at + c - lo : at + c - lo + P]
+            for m in range(lo, hi, P):
+                picked_planes[a, m] = plane[:, at + m - lo : at + m - lo + P]
 
-        def gather(a, lo, hi, t):
-            nc.vector.tensor_copy(t[:], tab_words[a][:].bitcast(U32).indirect(offsets[:, lo // PER_COL : hi // PER_COL]))
-            for c in range(lo, hi, P):
-                picked.setdefault((a, c), t[:, c - lo : c - lo + P])
+        def gather_words(a, lo, hi, picked):
+            window = tab_words[a][:].bitcast(U32)
+            nc.vector.tensor_copy(picked[:], window.indirect(offsets[:, lo // PER_COL : hi // PER_COL]))
+            for m in range(lo, hi, P):
+                picked_words.setdefault((a, m), picked[:, m - lo : m - lo + P])
 
-        raw0a = keep.tile([P, PACK, HALF], F32, name="raw0a", align_bytes=64)
-        raw0b = ring.tile([P, PACK, HALF], F32, name="raw0b", offset=at_raw0b, align_bytes=64)
+        raw0_first = keep.tile([P, PACK, HALF], F32, name="raw0_first", align_bytes=64)
+        raw0_second = reused.tile([P, PACK, HALF], F32, name="raw0_second", offset=at_raw0_second, align_bytes=64)
         nc.sync.dma_start(
-            tab_scales[ROW0:P, :].bitcast(I32),
+            scale_rows[ROW0:P, :].bitcast(I32),
             tab[:, WORD_BYTES : WORD_BYTES + BLOCKS * T].rearrange("a (q t) -> q a t", q=BLOCKS).bitcast(I32),
         )
         nc.sync.dma_start(offsets[:], offs)
         load_words(0)
-        load_w(0, 0, raw0a)
+        load_w(0, 0, raw0_first)
         load_words(1)
-        load_w(0, HALF, raw0b)
+        load_w(0, HALF, raw0_second)
 
-        nc.vector.memset(tab_scales[0:ROW0, :].bitcast(I32), 0)
-        early_plane = keep.tile([P, EARLY], U8, name="early_plane", align_bytes=64)
-        nc.vector.memset(early_plane[:].bitcast(I32), 0)
-        nc.vector.tensor_copy(picked_scales[:], tab_scales[:].indirect(offsets[:]))
-        move_scales(early_plane, 0, 0, 0, EARLY, 0)
+        nc.vector.memset(scale_rows[0:ROW0, :].bitcast(I32), 0)
+        early_planes = keep.tile([P, EARLY], U8, name="early_planes", align_bytes=64)
+        nc.vector.memset(early_planes[:].bitcast(I32), 0)
+        nc.vector.tensor_copy(picked_rows[:], scale_rows[:].indirect(offsets[:]))
+        move_to_plane(early_planes, 0, 0, 0, EARLY)
 
-        cuts = [0, HALF, M]
         raw1 = []
-        for n0, n1 in zip(cuts, cuts[1:]):
-            raw = ring.tile([P, PACK, n1 - n0], F32, name=f"raw1_{n0}", offset=at_scales + n0 * COL_RAW, align_bytes=64)
-            load_w(1, n0, raw)
-            raw1.append((n0, n1, raw))
+        for h in range(2):
+            raw = reused.tile(
+                [P, PACK, HALF], F32, name=f"raw1_{h}", offset=at_scale_rows + h * RAW_HALF_BYTES, align_bytes=64
+            )
+            load_w(1, h * HALF, raw)
+            raw1.append(raw)
 
-        gather(0, 0, N_LIST, keep.tile([P, N_LIST], U32, name="picked0", align_bytes=64))
-        bf0a = ring.tile([P, HALF, PACK], BF16, name="bf0a", offset=at_bf0a, align_bytes=64)
-        round_w(raw0a, bf0a[:])
-        quantise_w(0, 0, HALF, bf0a[:])
-        late_plane = ring.tile([P, 2 * N_LIST - EARLY], U8, name="late_plane", offset=at_bf0a, align_bytes=64)
-        nc.vector.memset(late_plane[:].bitcast(I32), 0)
-        move_scales(late_plane, 0, 0, EARLY, N_LIST, 0)
-        move_scales(late_plane, N_LIST - EARLY, 1, 0, N_LIST, 0)
+        gather_words(0, 0, N_LIST, keep.tile([P, N_LIST], U32, name="picked0", align_bytes=64))
+        rounded0_first = reused.tile(
+            [P, HALF, PACK], BF16, name="rounded0_first", offset=at_rounded0_first, align_bytes=64
+        )
+        round_w(raw0_first, rounded0_first[:])
+        quantise_w(0, 0, rounded0_first[:])
 
-        gather(1, 0, CUT1, keep.tile([P, CUT1], U32, name="picked1_first", align_bytes=64))
-        bf0b = keep.tile([P, HALF, PACK], BF16, name="bf0b", align_bytes=64)
-        round_w(raw0b, bf0b[:])
-        quantise_w(0, HALF, M, bf0b[:])
-        gather(1, CUT1, CUT2, ring.tile([P, CUT2 - CUT1], U32, name="picked1_middle", offset=at_raw0b, align_bytes=64))
-        bf1 = keep.tile([P, M, PACK], BF16, name="bf1", align_bytes=64)
-        for n0, n1, raw in raw1:
-            round_w(raw, bf1[:, n0:n1, :])
-        for n0, n1 in zip([0, HALF, M], [0, HALF, M][1:]):
-            quantise_w(1, n0, n1, bf1[:, n0:n1, :])
-        gather(1, LAST, N_LIST, ring.tile([P, S], U32, name="picked1_last", offset=at_scales + cuts[-2] * COL_RAW, align_bytes=64))
+        late_planes = reused.tile(
+            [P, PASSES * N_LIST - EARLY], U8, name="late_planes", offset=at_rounded0_first, align_bytes=64
+        )
+        nc.vector.memset(late_planes[:].bitcast(I32), 0)
+        move_to_plane(late_planes, 0, 0, EARLY, N_LIST)
+        move_to_plane(late_planes, N_LIST - EARLY, 1, 0, N_LIST)
+
+        gather_words(1, 0, FIRST_END, keep.tile([P, FIRST_END], U32, name="picked1_first", align_bytes=64))
+        rounded0_second = keep.tile([P, HALF, PACK], BF16, name="rounded0_second", align_bytes=64)
+        round_w(raw0_second, rounded0_second[:])
+        quantise_w(0, HALF, rounded0_second[:])
+        middle = reused.tile([P, S], U32, name="picked1_middle", offset=at_raw0_second, align_bytes=64)
+        gather_words(1, FIRST_END, MIDDLE_END, middle)
+        rounded1 = keep.tile([P, M, PACK], BF16, name="rounded1", align_bytes=64)
+        for h in range(2):
+            round_w(raw1[h], rounded1[:, h * HALF : (h + 1) * HALF, :])
+        for h in range(2):
+            quantise_w(1, h * HALF, rounded1[:, h * HALF : (h + 1) * HALF, :])
+        last = reused.tile([P, S], U32, name="picked1_last", offset=at_scale_rows + RAW_HALF_BYTES, align_bytes=64)
+        gather_words(1, LAST_START, N_LIST, last)
 
         banks = {}
         for j in range(S // P):
-            if j in SPLIT:
+            if j in TWO_BANKS:
                 for n0 in (0, HALF):
                     banks[j, n0] = (psum.tile([P, HALF], F32, name=f"acc{j}_{n0}"), n0)
             else:
                 banks[j, 0] = banks[j, HALF] = (psum.tile([P, M], F32, name=f"acc{j}"), 0)
 
-        def one_pass(a, g, j, n0, n1):
-            bank, first_col = banks[j, n0]
-            c = g * S + j * P
+        def multiply_columns(a, g, j, n0, n1):
+            bank, bank_col = banks[j, n0]
+            m = g * S + j * P
             nc.tensor.matmul_mx(
-                out=bank[:, n0 - first_col : n1 - first_col],
-                lhsT=picked[a, c].bitcast(FP8X4),
-                lhsT_scale=planes[a, c],
+                out=bank[:, n0 - bank_col : n1 - bank_col],
+                lhsT=picked_words[a, m].bitcast(FP8X4),
+                lhsT_scale=picked_planes[a, m],
                 rhs=w_codes[a][:, n0:n1].bitcast(FP8X4),
-                rhs_scale=w_scales[a][:, n0:n1],
-                start=(a == 0 and g == 0 and n0 == first_col),
+                rhs_scale=w_planes[a][:, n0:n1],
+                start=(a == 0 and g == 0 and n0 == bank_col),
                 stop=(a == PASSES - 1 and g == G - 1),
             )
 
         def multiply(a, g, j):
-            if j in SPLIT:
-                one_pass(a, g, j, 0, HALF)
-                one_pass(a, g, j, HALF, M)
+            if j in TWO_BANKS:
+                multiply_columns(a, g, j, 0, HALF)
+                multiply_columns(a, g, j, HALF, M)
             else:
-                one_pass(a, g, j, 0, M)
+                multiply_columns(a, g, j, 0, M)
 
-        for i, width in enumerate((512, 64)):
-            spare = psum.tile([P, width], F32, name=f"spare{i}")
+        for i, width in enumerate(WARM_UP_WIDTHS):
+            unread = psum.tile([P, width], F32, name=f"unread{i}")
             nc.tensor.matmul_mx(
-                out=spare[:],
+                out=unread[:],
                 lhsT=w_codes[0][:, 0:P].bitcast(FP8X4),
-                lhsT_scale=w_scales[0][:, 0:P],
+                lhsT_scale=w_planes[0][:, 0:P],
                 rhs=tab_words[1][:, 0:width].bitcast(FP8X4),
-                rhs_scale=picked_scales[:, 0:width],
+                rhs_scale=picked_rows[:, 0:width],
                 start=True,
                 stop=True,
             )
-        in_halves = [(j, 0) for j in range(S // P)] + [(1, 1), (0, 1)]
+
+        early_pairs = [(0, j) for j in range(S // P)] + [(1, 1), (1, 0)]
         for n0 in (0, HALF):
-            for j, g in in_halves:
-                one_pass(0, g, j, n0, n0 + HALF)
+            for g, j in early_pairs:
+                multiply_columns(0, g, j, n0, n0 + HALF)
         for g in range(G):
             for j in range(S // P):
-                if (j, g) not in in_halves:
+                if (g, j) not in early_pairs:
                     multiply(0, g, j)
-        for j, g in [(0, 0), (0, 1), (0, 2), (1, 0), (1, 1), (2, 0), (2, 1), (1, 2), (2, 2), (3, 0), (3, 1), (3, 2)]:
-            multiply(1, g, j)
+
+        for g in range(G - 1):
+            multiply_columns(1, g, 1, 0, HALF)
+        for g in range(G):
+            multiply(1, g, 0)
+        for g in range(G - 1):
+            multiply_columns(1, g, 1, HALF, M)
+        for g in range(G - 1):
+            multiply(1, g, 2)
+        for j in (1, 2):
+            multiply(1, G - 1, j)
+        for g in range(G):
+            multiply(1, g, 3)
 
         parts = []
         for j in range(S // P):
-            parts.extend([(j, 0, HALF), (j, HALF, M)] if j in SPLIT else [(j, 0, M)])
-        res = [keep.tile([P, M], F32, name=f"res{j}") for j in range(S // P)]
+            parts.extend([(j, 0, HALF), (j, HALF, M)] if j in TWO_BANKS else [(j, 0, M)])
+        result = [keep.tile([P, M], F32, name=f"result{j}") for j in range(S // P)]
         for i, (j, n0, n1) in enumerate(parts):
-            if "svsvsv"[i] == "s":
-                nc.scalar.copy(res[j][:, n0:n1], banks[j, n0][0][:])
+            if i % 2 == 0:
+                nc.scalar.copy(result[j][:, n0:n1], banks[j, n0][0][:])
             else:
-                nc.vector.tensor_copy(res[j][:, n0:n1], banks[j, n0][0][:])
+                nc.vector.tensor_copy(result[j][:, n0:n1], banks[j, n0][0][:])
             if n1 == M:
-                nc.sync.dma_start(out[j * P : (j + 1) * P, :], res[j][:])
+                nc.sync.dma_start(out[j * P : (j + 1) * P, :], result[j][:])

@@ -30,7 +30,7 @@ EARLY = N_LIST // 2
 FIRST_END = S + P
 MIDDLE_END = FIRST_END + S
 LAST_START = N_LIST - S
-TWO_BANKS = (1, 3)
+TWO_BANKS = (0, 1, 3)
 WARM_UP_WIDTHS = (512, 64)
 RAW_HALF_BYTES = PACK * HALF * 4
 
@@ -143,11 +143,23 @@ def tile_list_tabbag_tm_none_kernel(tc, tab, w, offs, out):
         last = reused.tile([P, S], U32, name="picked1_last", offset=at_scale_rows + RAW_HALF_BYTES, align_bytes=64)
         gather_words(1, LAST_START, N_LIST, last)
 
+        for width, tag in zip(WARM_UP_WIDTHS, ("unread", f"acc3_{HALF}")):
+            unread = psum.tile([P, width], F32, name=f"unread{width}", tag=tag)
+            nc.tensor.matmul_mx(
+                out=unread[:],
+                lhsT=w_codes[0][:, 0:P].bitcast(FP8X4),
+                lhsT_scale=w_planes[0][:, 0:P],
+                rhs=tab_words[1][:, 0:width].bitcast(FP8X4),
+                rhs_scale=picked_rows[:, 0:width],
+                start=True,
+                stop=True,
+            )
+
         banks = {}
         for j in range(S // P):
             if j in TWO_BANKS:
                 for n0 in (0, HALF):
-                    banks[j, n0] = (psum.tile([P, HALF], F32, name=f"acc{j}_{n0}"), n0)
+                    banks[j, n0] = (psum.tile([P, HALF], F32, name=f"acc{j}_{n0}", tag=f"acc{j}_{n0}"), n0)
             else:
                 banks[j, 0] = banks[j, HALF] = (psum.tile([P, M], F32, name=f"acc{j}"), 0)
 
@@ -171,18 +183,6 @@ def tile_list_tabbag_tm_none_kernel(tc, tab, w, offs, out):
             else:
                 multiply_columns(a, g, j, 0, M)
 
-        for i, width in enumerate(WARM_UP_WIDTHS):
-            unread = psum.tile([P, width], F32, name=f"unread{i}")
-            nc.tensor.matmul_mx(
-                out=unread[:],
-                lhsT=w_codes[0][:, 0:P].bitcast(FP8X4),
-                lhsT_scale=w_planes[0][:, 0:P],
-                rhs=tab_words[1][:, 0:width].bitcast(FP8X4),
-                rhs_scale=picked_rows[:, 0:width],
-                start=True,
-                stop=True,
-            )
-
         early_pairs = [(0, j) for j in range(S // P)] + [(1, 1), (1, 0)]
         for n0 in (0, HALF):
             for g, j in early_pairs:
@@ -192,14 +192,12 @@ def tile_list_tabbag_tm_none_kernel(tc, tab, w, offs, out):
                 if (g, j) not in early_pairs:
                     multiply(0, g, j)
 
-        for g in range(G - 1):
-            multiply_columns(1, g, 1, 0, HALF)
-        for g in range(G):
-            multiply(1, g, 0)
-        for g in range(G - 1):
-            multiply_columns(1, g, 1, HALF, M)
-        for g in range(G - 1):
-            multiply(1, g, 2)
+        for n0 in (0, HALF):
+            for g in range(G):
+                multiply_columns(1, g, 0, n0, n0 + HALF)
+        for j in (1, 2):
+            for g in range(G - 1):
+                multiply(1, g, j)
         for j in (1, 2):
             multiply(1, G - 1, j)
         for g in range(G):
@@ -210,7 +208,7 @@ def tile_list_tabbag_tm_none_kernel(tc, tab, w, offs, out):
             parts.extend([(j, 0, HALF), (j, HALF, M)] if j in TWO_BANKS else [(j, 0, M)])
         result = [keep.tile([P, M], F32, name=f"result{j}") for j in range(S // P)]
         for i, (j, n0, n1) in enumerate(parts):
-            if i % 2 == 0:
+            if j == 0 or i % 2 == 1:
                 nc.scalar.copy(result[j][:, n0:n1], banks[j, n0][0][:])
             else:
                 nc.vector.tensor_copy(result[j][:, n0:n1], banks[j, n0][0][:])

@@ -28,9 +28,9 @@ ROW0 = P - PASSES * BLOCKS
 
 EARLY = N_LIST // 2
 FIRST_END = S + P
-MIDDLE_END = FIRST_END + S
+MIDDLE_END = FIRST_END + S + P
 LAST_START = N_LIST - S
-TWO_BANKS = (0, 1, 3)
+TWO_BANKS = (0, 2, 3)
 WARM_UP_WIDTHS = (512, 64)
 RAW_HALF_BYTES = PACK * HALF * 4
 
@@ -133,7 +133,7 @@ def tile_list_tabbag_tm_none_kernel(tc, tab, w, offs, out):
         rounded0_second = keep.tile([P, HALF, PACK], BF16, name="rounded0_second", align_bytes=64)
         round_w(raw0_second, rounded0_second[:])
         quantise_w(0, HALF, rounded0_second[:])
-        middle = reused.tile([P, S], U32, name="picked1_middle", offset=at_raw0_second, align_bytes=64)
+        middle = reused.tile([P, MIDDLE_END - FIRST_END], U32, name="picked1_middle", offset=at_raw0_second, align_bytes=64)
         gather_words(1, FIRST_END, MIDDLE_END, middle)
         rounded1 = keep.tile([P, M, PACK], BF16, name="rounded1", align_bytes=64)
         for h in range(2):
@@ -195,20 +195,20 @@ def tile_list_tabbag_tm_none_kernel(tc, tab, w, offs, out):
         for n0 in (0, HALF):
             for g in range(G):
                 multiply_columns(1, g, 0, n0, n0 + HALF)
-        for j in (1, 2):
+        for g in range(G):
+            multiply(1, g, 1)
+        for j in (2, 3):
             for g in range(G - 1):
                 multiply(1, g, j)
-        for j in (1, 2):
+        for j in (2, 3):
             multiply(1, G - 1, j)
-        for g in range(G):
-            multiply(1, g, 3)
 
         parts = []
         for j in range(S // P):
             parts.extend([(j, 0, HALF), (j, HALF, M)] if j in TWO_BANKS else [(j, 0, M)])
         result = [keep.tile([P, M], F32, name=f"result{j}") for j in range(S // P)]
         for i, (j, n0, n1) in enumerate(parts):
-            if j == 0 or i % 2 == 1:
+            if j <= 1 or i % 2 == 0:
                 nc.scalar.copy(result[j][:, n0:n1], banks[j, n0][0][:])
             else:
                 nc.vector.tensor_copy(result[j][:, n0:n1], banks[j, n0][0][:])

@@ -31,7 +31,9 @@ FIRST_END = S + P
 MIDDLE_END = FIRST_END + S + P
 LAST_START = N_LIST - S
 TWO_BANKS = (0, 2, 3)
-WARM_UP_WIDTHS = (512, 64)
+WARM_UPS = 4
+WARM_UP_ROWS = 32
+WARM_UP_WIDTH = 512
 RAW_HALF_BYTES = PACK * HALF * 4
 
 
@@ -115,7 +117,8 @@ def tile_list_tabbag_tm_none_kernel(tc, tab, w, offs, out):
             load_w(1, h * HALF, raw)
             raw1.append(raw)
 
-        gather_words(0, 0, N_LIST, keep.tile([P, N_LIST], U32, name="picked0", align_bytes=64))
+        picked0 = keep.tile([P, N_LIST], U32, name="picked0", align_bytes=64)
+        gather_words(0, 0, N_LIST, picked0)
         rounded0_first = reused.tile(
             [P, HALF, PACK], BF16, name="rounded0_first", offset=at_rounded0_first, align_bytes=64
         )
@@ -143,14 +146,14 @@ def tile_list_tabbag_tm_none_kernel(tc, tab, w, offs, out):
         last = reused.tile([P, S], U32, name="picked1_last", offset=at_scale_rows + RAW_HALF_BYTES, align_bytes=64)
         gather_words(1, LAST_START, N_LIST, last)
 
-        for width, tag in zip(WARM_UP_WIDTHS, ("unread", f"acc3_{HALF}")):
-            unread = psum.tile([P, width], F32, name=f"unread{width}", tag=tag)
+        unread = psum.tile([WARM_UP_ROWS, WARM_UP_WIDTH], F32, name="unread")
+        for i in range(WARM_UPS):
             nc.tensor.matmul_mx(
                 out=unread[:],
-                lhsT=w_codes[0][:, 0:P].bitcast(FP8X4),
-                lhsT_scale=w_planes[0][:, 0:P],
-                rhs=tab_words[1][:, 0:width].bitcast(FP8X4),
-                rhs_scale=picked_rows[:, 0:width],
+                lhsT=w_codes[0][:, 0:WARM_UP_ROWS].bitcast(FP8X4),
+                lhsT_scale=w_planes[0][:, 0:WARM_UP_ROWS],
+                rhs=picked0[:, 0:WARM_UP_WIDTH].bitcast(FP8X4),
+                rhs_scale=picked_rows[:, 0:WARM_UP_WIDTH],
                 start=True,
                 stop=True,
             )

@@ -30,7 +30,7 @@ EARLY = N_LIST // 2
 FIRST_END = S + P
 MIDDLE_END = FIRST_END + S + P
 LAST_START = N_LIST - S
-TWO_BANKS = (0, 2, 3)
+TWO_BANKS = (2, 3)
 WARM_UPS = 4
 WARM_UP_ROWS = 32
 WARM_UP_WIDTH = 512
@@ -186,7 +186,7 @@ def tile_list_tabbag_tm_none_kernel(tc, tab, w, offs, out):
             else:
                 multiply_columns(a, g, j, 0, M)
 
-        early_pairs = [(0, j) for j in range(S // P)] + [(1, 1), (1, 0)]
+        early_pairs = [(m // S, m % S // P) for m in range(0, EARLY, P)]
         for n0 in (0, HALF):
             for g, j in early_pairs:
                 multiply_columns(0, g, j, n0, n0 + HALF)
@@ -195,14 +195,15 @@ def tile_list_tabbag_tm_none_kernel(tc, tab, w, offs, out):
                 if (g, j) not in early_pairs:
                     multiply(0, g, j)
 
-        for n0 in (0, HALF):
+        for g in range(G - 1):
+            multiply_columns(1, g, 2, 0, HALF)
+        for j in (0, 1):
             for g in range(G):
-                multiply_columns(1, g, 0, n0, n0 + HALF)
-        for g in range(G):
-            multiply(1, g, 1)
-        for j in (2, 3):
-            for g in range(G - 1):
                 multiply(1, g, j)
+        for g in range(G - 1):
+            multiply_columns(1, g, 2, HALF, M)
+        for g in range(G - 1):
+            multiply(1, g, 3)
         for j in (2, 3):
             multiply(1, G - 1, j)
 
@@ -211,7 +212,7 @@ def tile_list_tabbag_tm_none_kernel(tc, tab, w, offs, out):
             parts.extend([(j, 0, HALF), (j, HALF, M)] if j in TWO_BANKS else [(j, 0, M)])
         result = [keep.tile([P, M], F32, name=f"result{j}") for j in range(S // P)]
         for i, (j, n0, n1) in enumerate(parts):
-            if j <= 1 or i % 2 == 0:
+            if j <= 1 or i % 2 == 1:
                 nc.scalar.copy(result[j][:, n0:n1], banks[j, n0][0][:])
             else:
                 nc.vector.tensor_copy(result[j][:, n0:n1], banks[j, n0][0][:])

@@ -18,6 +18,7 @@ PACK = 4
 K_PASS = P * PACK
 PASSES = K // K_PASS
 N_LIST = G * S
+ROW_BLOCKS = S // P
 PER_COL = 16
 WORD_BYTES = K_PASS * T
 BLOCKS = K_PASS // 32
@@ -25,16 +26,13 @@ QUADRANT = 32
 LIVE_ROWS = 4
 HALF = M // 2
 ROW0 = P - PASSES * BLOCKS
+RAW_BYTES = PACK * HALF * 4
 
-EARLY = N_LIST // 2
-FIRST_END = S + P
-MIDDLE_END = FIRST_END + S + P
-LAST_START = N_LIST - S
-TWO_BANKS = (2, 3)
+CUTS = (0, 512, 896, 1152, N_LIST)
+WARM_AFTER = 1024
 WARM_UPS = 4
 WARM_UP_ROWS = 32
 WARM_UP_WIDTH = 512
-RAW_HALF_BYTES = PACK * HALF * 4
 
 
 def tile_list_tabbag_tm_none_kernel(tc, tab, w, offs, out):
@@ -44,9 +42,9 @@ def tile_list_tabbag_tm_none_kernel(tc, tab, w, offs, out):
         reused = ctx.enter_context(tc.tile_pool(name="reused", bufs=1))
         psum = ctx.enter_context(tc.psum_pool(name="psum", bufs=1))
 
-        at_scale_rows = 0
-        at_raw0_second = 2 * T
-        at_rounded0_first = 3 * T
+        halves = [(a, n0) for a in range(PASSES) for n0 in (0, HALF)]
+        at_raw = {half: i * RAW_BYTES for i, half in enumerate(halves)}
+        at_scale_rows = RAW_BYTES + RAW_BYTES // 2
 
         offsets = keep.tile([P, N_LIST // PER_COL], U16, name="offsets")
         scale_rows = reused.tile([P, T], U8, name="scale_rows", offset=at_scale_rows, align_bytes=64)
@@ -54,167 +52,117 @@ def tile_list_tabbag_tm_none_kernel(tc, tab, w, offs, out):
         w_codes = [keep.tile([P, M], U32, name=f"w_codes{a}", align_bytes=64) for a in range(PASSES)]
         w_planes = [keep.tile([P, M], U8, name=f"w_planes{a}", align_bytes=64) for a in range(PASSES)]
         picked_rows = keep.tile([P, N_LIST], U8, name="picked_rows", align_bytes=64)
+        planes = keep.tile([P, PASSES * N_LIST], U8, name="planes", align_bytes=64)
         picked_words = {}
-        picked_planes = {}
+        raw = {}
 
         def load_words(a):
             nc.sync.dma_start(tab_words[a][:], tab[a, 0:WORD_BYTES].rearrange("(p b) -> p b", p=P).bitcast(I32))
 
-        def load_w(a, n0, raw):
+        def load_w(a, n0):
+            raw[a, n0] = reused.tile([P, PACK, HALF], F32, name=f"raw{a}_{n0}", offset=at_raw[a, n0], align_bytes=64)
             rows = w[a * K_PASS : (a + 1) * K_PASS, :].rearrange("(p t) n -> p t n", t=PACK)
-            nc.sync.dma_start(raw[:], rows[:, :, n0 : n0 + HALF])
+            nc.sync.dma_start(raw[a, n0][:], rows[:, :, n0 : n0 + HALF])
 
-        def round_w(raw, rounded):
+        def quantise_w(a, n0):
+            rounded = keep.tile([P, HALF, PACK], BF16, name=f"rounded{a}_{n0}", align_bytes=64)
             nc.scalar.copy(
-                rounded.rearrange("p (c e) t -> p c t e", e=4), raw[:].rearrange("p t (c e) -> p c t e", e=4)
+                rounded[:].rearrange("p (c e) t -> p c t e", e=4),
+                raw[a, n0][:].rearrange("p t (c e) -> p c t e", e=4),
             )
-
-        def quantise_w(a, n0, rounded):
             nc.vector.quantize_mx(
                 out=w_codes[a][:, n0 : n0 + HALF].bitcast(FP8X4),
                 scales=w_planes[a][:, n0 : n0 + HALF],
-                in_=rounded.rearrange("p n t -> p (n t)"),
+                in_=rounded[:].rearrange("p n t -> p (n t)"),
             )
 
-        def move_to_plane(plane, at, a, lo, hi):
+        def move_to_plane(a):
             for r in range(LIVE_ROWS):
                 nc.sync.dma_start(
-                    plane[r:P:QUADRANT, at : at + hi - lo].bitcast(I32),
-                    picked_rows[ROW0 + PASSES * r + a : P : PASSES * LIVE_ROWS, lo:hi].bitcast(I32),
+                    planes[r:P:QUADRANT, a * N_LIST : (a + 1) * N_LIST].bitcast(I32),
+                    picked_rows[ROW0 + PASSES * r + a : P : PASSES * LIVE_ROWS, :].bitcast(I32),
                 )
-            for m in range(lo, hi, P):
-                picked_planes[a, m] = plane[:, at + m - lo : at + m - lo + P]
 
         def gather_words(a, lo, hi, picked):
             window = tab_words[a][:].bitcast(U32)
             nc.vector.tensor_copy(picked[:], window.indirect(offsets[:, lo // PER_COL : hi // PER_COL]))
             for m in range(lo, hi, P):
-                picked_words.setdefault((a, m), picked[:, m - lo : m - lo + P])
+                picked_words[a, m] = picked[:, m - lo : m - lo + P]
 
-        raw0_first = keep.tile([P, PACK, HALF], F32, name="raw0_first", align_bytes=64)
-        raw0_second = reused.tile([P, PACK, HALF], F32, name="raw0_second", offset=at_raw0_second, align_bytes=64)
         nc.sync.dma_start(
             scale_rows[ROW0:P, :].bitcast(I32),
             tab[:, WORD_BYTES : WORD_BYTES + BLOCKS * T].rearrange("a (q t) -> q a t", q=BLOCKS).bitcast(I32),
         )
         nc.sync.dma_start(offsets[:], offs)
         load_words(0)
-        load_w(0, 0, raw0_first)
         load_words(1)
-        load_w(0, HALF, raw0_second)
+        load_w(0, 0)
 
         nc.vector.memset(scale_rows[0:ROW0, :].bitcast(I32), 0)
-        early_planes = keep.tile([P, EARLY], U8, name="early_planes", align_bytes=64)
-        nc.vector.memset(early_planes[:].bitcast(I32), 0)
+        nc.vector.memset(planes[:].bitcast(I32), 0)
         nc.vector.tensor_copy(picked_rows[:], scale_rows[:].indirect(offsets[:]))
-        move_to_plane(early_planes, 0, 0, 0, EARLY)
 
-        raw1 = []
-        for h in range(2):
-            raw = reused.tile(
-                [P, PACK, HALF], F32, name=f"raw1_{h}", offset=at_scale_rows + h * RAW_HALF_BYTES, align_bytes=64
-            )
-            load_w(1, h * HALF, raw)
-            raw1.append(raw)
+        move_to_plane(0)
+        load_w(0, HALF)
+        load_w(1, 0)
+        move_to_plane(1)
+        load_w(1, HALF)
 
-        picked0 = keep.tile([P, N_LIST], U32, name="picked0", align_bytes=64)
-        gather_words(0, 0, N_LIST, picked0)
-        rounded0_first = reused.tile(
-            [P, HALF, PACK], BF16, name="rounded0_first", offset=at_rounded0_first, align_bytes=64
-        )
-        round_w(raw0_first, rounded0_first[:])
-        quantise_w(0, 0, rounded0_first[:])
+        picked0_first = keep.tile([P, WARM_AFTER], U32, name="picked0_first", align_bytes=64)
+        gather_words(0, 0, WARM_AFTER, picked0_first)
+        gather_words(0, WARM_AFTER, N_LIST, keep.tile([P, N_LIST - WARM_AFTER], U32, name="picked0_rest", align_bytes=64))
 
-        late_planes = reused.tile(
-            [P, PASSES * N_LIST - EARLY], U8, name="late_planes", offset=at_rounded0_first, align_bytes=64
-        )
-        nc.vector.memset(late_planes[:].bitcast(I32), 0)
-        move_to_plane(late_planes, 0, 0, EARLY, N_LIST)
-        move_to_plane(late_planes, N_LIST - EARLY, 1, 0, N_LIST)
+        for i, (a, n0) in enumerate(halves):
+            lo, hi = CUTS[i], CUTS[i + 1]
+            if i == 0:
+                piece = keep.tile([P, hi - lo], U32, name="picked1_0", align_bytes=64)
+            else:
+                piece = reused.tile([P, hi - lo], U32, name=f"picked1_{i}", offset=at_raw[halves[i - 1]], align_bytes=64)
+            gather_words(1, lo, hi, piece)
+            quantise_w(a, n0)
 
-        gather_words(1, 0, FIRST_END, keep.tile([P, FIRST_END], U32, name="picked1_first", align_bytes=64))
-        rounded0_second = keep.tile([P, HALF, PACK], BF16, name="rounded0_second", align_bytes=64)
-        round_w(raw0_second, rounded0_second[:])
-        quantise_w(0, HALF, rounded0_second[:])
-        middle = reused.tile([P, MIDDLE_END - FIRST_END], U32, name="picked1_middle", offset=at_raw0_second, align_bytes=64)
-        gather_words(1, FIRST_END, MIDDLE_END, middle)
-        rounded1 = keep.tile([P, M, PACK], BF16, name="rounded1", align_bytes=64)
-        for h in range(2):
-            round_w(raw1[h], rounded1[:, h * HALF : (h + 1) * HALF, :])
-        for h in range(2):
-            quantise_w(1, h * HALF, rounded1[:, h * HALF : (h + 1) * HALF, :])
-        last = reused.tile([P, S], U32, name="picked1_last", offset=at_scale_rows + RAW_HALF_BYTES, align_bytes=64)
-        gather_words(1, LAST_START, N_LIST, last)
-
-        unread = psum.tile([WARM_UP_ROWS, WARM_UP_WIDTH], F32, name="unread")
+        unread = psum.tile([WARM_UP_ROWS, WARM_UP_WIDTH], F32, name="unread", tag="last_bank")
         for i in range(WARM_UPS):
             nc.tensor.matmul_mx(
                 out=unread[:],
-                lhsT=w_codes[0][:, 0:WARM_UP_ROWS].bitcast(FP8X4),
-                lhsT_scale=w_planes[0][:, 0:WARM_UP_ROWS],
-                rhs=picked0[:, 0:WARM_UP_WIDTH].bitcast(FP8X4),
+                lhsT=picked0_first[:, 0:WARM_UP_ROWS].bitcast(FP8X4),
+                lhsT_scale=picked_rows[:, 0:WARM_UP_ROWS],
+                rhs=picked0_first[:, 0:WARM_UP_WIDTH].bitcast(FP8X4),
                 rhs_scale=picked_rows[:, 0:WARM_UP_WIDTH],
                 start=True,
                 stop=True,
             )
 
         banks = {}
-        for j in range(S // P):
-            if j in TWO_BANKS:
-                for n0 in (0, HALF):
-                    banks[j, n0] = (psum.tile([P, HALF], F32, name=f"acc{j}_{n0}", tag=f"acc{j}_{n0}"), n0)
-            else:
-                banks[j, 0] = banks[j, HALF] = (psum.tile([P, M], F32, name=f"acc{j}"), 0)
+        for n0 in (0, HALF):
+            for j in range(ROW_BLOCKS):
+                tag = "last_bank" if (j, n0) == (ROW_BLOCKS - 1, HALF) else f"acc{j}_{n0}"
+                banks[j, n0] = psum.tile([P, HALF], F32, name=f"acc{j}_{n0}", tag=tag)
 
-        def multiply_columns(a, g, j, n0, n1):
-            bank, bank_col = banks[j, n0]
+        def multiply(a, n0, g, j):
             m = g * S + j * P
             nc.tensor.matmul_mx(
-                out=bank[:, n0 - bank_col : n1 - bank_col],
+                out=banks[j, n0][:],
                 lhsT=picked_words[a, m].bitcast(FP8X4),
-                lhsT_scale=picked_planes[a, m],
-                rhs=w_codes[a][:, n0:n1].bitcast(FP8X4),
-                rhs_scale=w_planes[a][:, n0:n1],
-                start=(a == 0 and g == 0 and n0 == bank_col),
+                lhsT_scale=planes[:, a * N_LIST + m : a * N_LIST + m + P],
+                rhs=w_codes[a][:, n0 : n0 + HALF].bitcast(FP8X4),
+                rhs_scale=w_planes[a][:, n0 : n0 + HALF],
+                start=(a == 0 and g == 0),
                 stop=(a == PASSES - 1 and g == G - 1),
             )
 
-        def multiply(a, g, j):
-            if j in TWO_BANKS:
-                multiply_columns(a, g, j, 0, HALF)
-                multiply_columns(a, g, j, HALF, M)
-            else:
-                multiply_columns(a, g, j, 0, M)
-
-        early_pairs = [(m // S, m % S // P) for m in range(0, EARLY, P)]
-        for n0 in (0, HALF):
-            for g, j in early_pairs:
-                multiply_columns(0, g, j, n0, n0 + HALF)
-        for g in range(G):
-            for j in range(S // P):
-                if (g, j) not in early_pairs:
-                    multiply(0, g, j)
-
-        for g in range(G - 1):
-            multiply_columns(1, g, 2, 0, HALF)
-        for j in (0, 1):
+        for a, n0 in halves[:-1]:
             for g in range(G):
-                multiply(1, g, j)
-        for g in range(G - 1):
-            multiply_columns(1, g, 2, HALF, M)
-        for g in range(G - 1):
-            multiply(1, g, 3)
-        for j in (2, 3):
-            multiply(1, G - 1, j)
+                for j in range(ROW_BLOCKS):
+                    multiply(a, n0, g, j)
+        for j in range(ROW_BLOCKS):
+            for g in range(G):
+                multiply(PASSES - 1, HALF, g, j)
 
-        parts = []
-        for j in range(S // P):
-            parts.extend([(j, 0, HALF), (j, HALF, M)] if j in TWO_BANKS else [(j, 0, M)])
-        result = [keep.tile([P, M], F32, name=f"result{j}") for j in range(S // P)]
-        for i, (j, n0, n1) in enumerate(parts):
-            if j <= 1 or i % 2 == 1:
-                nc.scalar.copy(result[j][:, n0:n1], banks[j, n0][0][:])
-            else:
-                nc.vector.tensor_copy(result[j][:, n0:n1], banks[j, n0][0][:])
-            if n1 == M:
-                nc.sync.dma_start(out[j * P : (j + 1) * P, :], result[j][:])
+        result = [keep.tile([P, M], F32, name=f"result{j}") for j in range(ROW_BLOCKS)]
+        for j in range(ROW_BLOCKS):
+            nc.scalar.copy(result[j][:, 0:HALF], banks[j, 0][:])
+            nc.sync.dma_start(out[j * P : (j + 1) * P, 0:HALF], result[j][:, 0:HALF])
+        for j in range(ROW_BLOCKS):
+            nc.vector.tensor_copy(result[j][:, HALF:M], banks[j, HALF][:])
+            nc.sync.dma_start(out[j * P : (j + 1) * P, HALF:M], result[j][:, HALF:M])

@@ -28,8 +28,9 @@ HALF = M // 2
 ROW0 = P - PASSES * BLOCKS
 RAW_BYTES = PACK * HALF * 4
 
-CUTS = (0, 512, 896, 1152, N_LIST)
-WARM_AFTER = 1024
+CUTS = (0, 640, 1024, 1280, N_LIST)
+NARROW = (1152, 1280)
+WARM_AFTER = 1280
 WARM_UPS = 4
 WARM_UP_ROWS = 32
 WARM_UP_WIDTH = 512
@@ -44,7 +45,7 @@ def tile_list_tabbag_tm_none_kernel(tc, tab, w, offs, out):
 
         halves = [(a, n0) for a in range(PASSES) for n0 in (0, HALF)]
         at_raw = {half: i * RAW_BYTES for i, half in enumerate(halves)}
-        at_scale_rows = RAW_BYTES + RAW_BYTES // 2
+        at_scale_rows = 2 * RAW_BYTES
 
         offsets = keep.tile([P, N_LIST // PER_COL], U16, name="offsets")
         scale_rows = reused.tile([P, T], U8, name="scale_rows", offset=at_scale_rows, align_bytes=64)
@@ -76,11 +77,11 @@ def tile_list_tabbag_tm_none_kernel(tc, tab, w, offs, out):
                 in_=rounded[:].rearrange("p n t -> p (n t)"),
             )
 
-        def move_to_plane(a):
+        def move_to_plane(a, lo, hi):
             for r in range(LIVE_ROWS):
                 nc.sync.dma_start(
-                    planes[r:P:QUADRANT, a * N_LIST : (a + 1) * N_LIST].bitcast(I32),
-                    picked_rows[ROW0 + PASSES * r + a : P : PASSES * LIVE_ROWS, :].bitcast(I32),
+                    planes[r:P:QUADRANT, a * N_LIST + lo : a * N_LIST + hi].bitcast(I32),
+                    picked_rows[ROW0 + PASSES * r + a : P : PASSES * LIVE_ROWS, lo:hi].bitcast(I32),
                 )
 
         def gather_words(a, lo, hi, picked):
@@ -95,31 +96,35 @@ def tile_list_tabbag_tm_none_kernel(tc, tab, w, offs, out):
         )
         nc.sync.dma_start(offsets[:], offs)
         load_words(0)
-        load_words(1)
         load_w(0, 0)
+        load_words(1)
+        load_w(0, HALF)
 
         nc.vector.memset(scale_rows[0:ROW0, :].bitcast(I32), 0)
         nc.vector.memset(planes[:].bitcast(I32), 0)
         nc.vector.tensor_copy(picked_rows[:], scale_rows[:].indirect(offsets[:]))
 
-        move_to_plane(0)
-        load_w(0, HALF)
+        move_to_plane(0, 0, N_LIST)
         load_w(1, 0)
-        move_to_plane(1)
         load_w(1, HALF)
+        move_to_plane(1, 0, CUTS[-2])
+        move_to_plane(1, CUTS[-2], N_LIST)
 
         picked0_first = keep.tile([P, WARM_AFTER], U32, name="picked0_first", align_bytes=64)
         gather_words(0, 0, WARM_AFTER, picked0_first)
         gather_words(0, WARM_AFTER, N_LIST, keep.tile([P, N_LIST - WARM_AFTER], U32, name="picked0_rest", align_bytes=64))
 
-        for i, (a, n0) in enumerate(halves):
+        quantise_w(0, 0)
+
+        for i in range(len(CUTS) - 1):
             lo, hi = CUTS[i], CUTS[i + 1]
             if i == 0:
                 piece = keep.tile([P, hi - lo], U32, name="picked1_0", align_bytes=64)
             else:
-                piece = reused.tile([P, hi - lo], U32, name=f"picked1_{i}", offset=at_raw[halves[i - 1]], align_bytes=64)
+                piece = reused.tile([P, hi - lo], U32, name=f"picked1_{i}", offset=at_raw[halves[i]], align_bytes=64)
             gather_words(1, lo, hi, piece)
-            quantise_w(a, n0)
+            if i + 1 < len(halves):
+                quantise_w(*halves[i + 1])
 
         unread = psum.tile([WARM_UP_ROWS, WARM_UP_WIDTH], F32, name="unread", tag="last_bank")
         for i in range(WARM_UPS):
@@ -133,36 +138,43 @@ def tile_list_tabbag_tm_none_kernel(tc, tab, w, offs, out):
                 stop=True,
             )
 
-        banks = {}
-        for n0 in (0, HALF):
-            for j in range(ROW_BLOCKS):
-                tag = "last_bank" if (j, n0) == (ROW_BLOCKS - 1, HALF) else f"acc{j}_{n0}"
-                banks[j, n0] = psum.tile([P, HALF], F32, name=f"acc{j}_{n0}", tag=tag)
+        banks = [
+            psum.tile([P, M], F32, name=f"acc{j}", tag="last_bank" if j == ROW_BLOCKS - 1 else f"acc{j}")
+            for j in range(ROW_BLOCKS)
+        ]
 
-        def multiply(a, n0, g, j):
-            m = g * S + j * P
+        def multiply(a, m, n0, n1):
+            g, j = m // S, m % S // P
             nc.tensor.matmul_mx(
-                out=banks[j, n0][:],
+                out=banks[j][:, n0:n1],
                 lhsT=picked_words[a, m].bitcast(FP8X4),
                 lhsT_scale=planes[:, a * N_LIST + m : a * N_LIST + m + P],
-                rhs=w_codes[a][:, n0 : n0 + HALF].bitcast(FP8X4),
-                rhs_scale=w_planes[a][:, n0 : n0 + HALF],
-                start=(a == 0 and g == 0),
-                stop=(a == PASSES - 1 and g == G - 1),
+                rhs=w_codes[a][:, n0:n1].bitcast(FP8X4),
+                rhs_scale=w_planes[a][:, n0:n1],
+                start=(a == 0 and g == 0 and n0 == 0),
+                stop=(a == PASSES - 1 and g == G - 1 and n1 == M),
             )
 
-        for a, n0 in halves[:-1]:
-            for g in range(G):
-                for j in range(ROW_BLOCKS):
-                    multiply(a, n0, g, j)
+        for n0 in (0, HALF):
+            for m in range(0, NARROW[0], P):
+                multiply(0, m, n0, n0 + HALF)
+        for m in range(NARROW[0], N_LIST, P):
+            multiply(0, m, 0, M)
+        for m in range(0, NARROW[1], P):
+            multiply(1, m, 0, HALF)
         for j in range(ROW_BLOCKS):
-            for g in range(G):
-                multiply(PASSES - 1, HALF, g, j)
+            for m in range(j * P, NARROW[1], S):
+                multiply(1, m, HALF, M)
+        for m in range(NARROW[1], N_LIST, P):
+            multiply(1, m, 0, M)
 
-        result = [keep.tile([P, M], F32, name=f"result{j}") for j in range(ROW_BLOCKS)]
+        results = reused.tile(
+            [P, ROW_BLOCKS * M], F32, name="results", offset=at_raw[halves[-1]] + RAW_BYTES // 2, align_bytes=64
+        )
         for j in range(ROW_BLOCKS):
-            nc.scalar.copy(result[j][:, 0:HALF], banks[j, 0][:])
-            nc.sync.dma_start(out[j * P : (j + 1) * P, 0:HALF], result[j][:, 0:HALF])
-        for j in range(ROW_BLOCKS):
-            nc.vector.tensor_copy(result[j][:, HALF:M], banks[j, HALF][:])
-            nc.sync.dma_start(out[j * P : (j + 1) * P, HALF:M], result[j][:, HALF:M])
+            result = results[:, j * M : (j + 1) * M]
+            if j < ROW_BLOCKS - 1:
+                nc.scalar.copy(result, banks[j][:])
+            else:
+                nc.vector.tensor_copy(result, banks[j][:])
+            nc.sync.dma_start(out[j * P : (j + 1) * P, :], result)

@@ -28,13 +28,9 @@ HALF = M // 2
 ROW0 = P - PASSES * BLOCKS
 RAW_BYTES = PACK * HALF * 4
 
-CUTS = (0, 640, 1024, 1280, N_LIST)
-NARROW = (1152, 1280)
-WARM_AFTER = 1280
-WARM_UPS = 4
-WARM_UP_ROWS = 32
-WARM_UP_WIDTH = 512
-
+CUTS = (0, 768, 1024, 1280, N_LIST)
+NARROW = 1024
+WARM_UP_WIDTHS = (512, 64)
 
 def tile_list_tabbag_tm_none_kernel(tc, tab, w, offs, out):
     nc = tc.nc
@@ -45,7 +41,7 @@ def tile_list_tabbag_tm_none_kernel(tc, tab, w, offs, out):
 
         halves = [(a, n0) for a in range(PASSES) for n0 in (0, HALF)]
         at_raw = {half: i * RAW_BYTES for i, half in enumerate(halves)}
-        at_scale_rows = 2 * RAW_BYTES
+        at_scale_rows = RAW_BYTES + RAW_BYTES // 2
 
         offsets = keep.tile([P, N_LIST // PER_COL], U16, name="offsets")
         scale_rows = reused.tile([P, T], U8, name="scale_rows", offset=at_scale_rows, align_bytes=64)
@@ -98,22 +94,19 @@ def tile_list_tabbag_tm_none_kernel(tc, tab, w, offs, out):
         load_words(0)
         load_w(0, 0)
         load_words(1)
-        load_w(0, HALF)
 
         nc.vector.memset(scale_rows[0:ROW0, :].bitcast(I32), 0)
         nc.vector.memset(planes[:].bitcast(I32), 0)
         nc.vector.tensor_copy(picked_rows[:], scale_rows[:].indirect(offsets[:]))
 
         move_to_plane(0, 0, N_LIST)
+        load_w(0, HALF)
         load_w(1, 0)
         load_w(1, HALF)
         move_to_plane(1, 0, CUTS[-2])
         move_to_plane(1, CUTS[-2], N_LIST)
 
-        picked0_first = keep.tile([P, WARM_AFTER], U32, name="picked0_first", align_bytes=64)
-        gather_words(0, 0, WARM_AFTER, picked0_first)
-        gather_words(0, WARM_AFTER, N_LIST, keep.tile([P, N_LIST - WARM_AFTER], U32, name="picked0_rest", align_bytes=64))
-
+        gather_words(0, 0, N_LIST, keep.tile([P, N_LIST], U32, name="picked0", align_bytes=64))
         quantise_w(0, 0)
 
         for i in range(len(CUTS) - 1):
@@ -126,55 +119,63 @@ def tile_list_tabbag_tm_none_kernel(tc, tab, w, offs, out):
             if i + 1 < len(halves):
                 quantise_w(*halves[i + 1])
 
-        unread = psum.tile([WARM_UP_ROWS, WARM_UP_WIDTH], F32, name="unread", tag="last_bank")
-        for i in range(WARM_UPS):
+        for width in WARM_UP_WIDTHS:
+            unread = psum.tile([P, width], F32, name=f"unread{width}")
             nc.tensor.matmul_mx(
                 out=unread[:],
-                lhsT=picked0_first[:, 0:WARM_UP_ROWS].bitcast(FP8X4),
-                lhsT_scale=picked_rows[:, 0:WARM_UP_ROWS],
-                rhs=picked0_first[:, 0:WARM_UP_WIDTH].bitcast(FP8X4),
-                rhs_scale=picked_rows[:, 0:WARM_UP_WIDTH],
+                lhsT=w_codes[0][:, 0:HALF].bitcast(FP8X4),
+                lhsT_scale=w_planes[0][:, 0:HALF],
+                rhs=tab_words[1][:, 0:width].bitcast(FP8X4),
+                rhs_scale=picked_rows[:, 0:width],
                 start=True,
                 stop=True,
             )
 
-        banks = [
-            psum.tile([P, M], F32, name=f"acc{j}", tag="last_bank" if j == ROW_BLOCKS - 1 else f"acc{j}")
-            for j in range(ROW_BLOCKS)
-        ]
+        last = ROW_BLOCKS - 1
+        banks = {}
+        for j in range(last):
+            banks[j, 0] = banks[j, HALF] = (psum.tile([P, M], F32, name=f"acc{j}"), 0)
+        for n0 in (0, HALF):
+            banks[last, n0] = (psum.tile([P, HALF], F32, name=f"acc{last}_{n0}"), n0)
 
         def multiply(a, m, n0, n1):
             g, j = m // S, m % S // P
+            if j == last and n1 - n0 == M:
+                multiply(a, m, 0, HALF)
+                multiply(a, m, HALF, M)
+                return
+            bank, bank_col = banks[j, n0]
             nc.tensor.matmul_mx(
-                out=banks[j][:, n0:n1],
+                out=bank[:, n0 - bank_col : n1 - bank_col],
                 lhsT=picked_words[a, m].bitcast(FP8X4),
                 lhsT_scale=planes[:, a * N_LIST + m : a * N_LIST + m + P],
                 rhs=w_codes[a][:, n0:n1].bitcast(FP8X4),
                 rhs_scale=w_planes[a][:, n0:n1],
-                start=(a == 0 and g == 0 and n0 == 0),
-                stop=(a == PASSES - 1 and g == G - 1 and n1 == M),
+                start=(a == 0 and g == 0 and n0 == bank_col),
+                stop=(a == PASSES - 1 and g == G - 1 and (n1 == M or j == last)),
             )
 
         for n0 in (0, HALF):
-            for m in range(0, NARROW[0], P):
+            for m in range(0, N_LIST, P):
                 multiply(0, m, n0, n0 + HALF)
-        for m in range(NARROW[0], N_LIST, P):
-            multiply(0, m, 0, M)
-        for m in range(0, NARROW[1], P):
+        for m in range(0, NARROW, P):
             multiply(1, m, 0, HALF)
         for j in range(ROW_BLOCKS):
-            for m in range(j * P, NARROW[1], S):
-                multiply(1, m, HALF, M)
-        for m in range(NARROW[1], N_LIST, P):
-            multiply(1, m, 0, M)
+            if j == last:
+                multiply(1, N_LIST - P, 0, HALF)
+            for m in range(j * P, N_LIST, S):
+                multiply(1, m, HALF if m < NARROW or j == last else 0, M)
 
         results = reused.tile(
             [P, ROW_BLOCKS * M], F32, name="results", offset=at_raw[halves[-1]] + RAW_BYTES // 2, align_bytes=64
         )
         for j in range(ROW_BLOCKS):
             result = results[:, j * M : (j + 1) * M]
-            if j < ROW_BLOCKS - 1:
-                nc.scalar.copy(result, banks[j][:])
+            if j == last:
+                for n0 in (0, HALF):
+                    nc.vector.tensor_copy(result[:, n0 : n0 + HALF], banks[j, n0][0][:])
+            elif j % 2 == 0:
+                nc.scalar.copy(result, banks[j, 0][0][:])
             else:
-                nc.vector.tensor_copy(result, banks[j][:])
+                nc.vector.tensor_copy(result, banks[j, 0][0][:])
             nc.sync.dma_start(out[j * P : (j + 1) * P, :], result)

@@ -28,9 +28,10 @@ HALF = M // 2
 ROW0 = P - PASSES * BLOCKS
 RAW_BYTES = PACK * HALF * 4
 
-CUTS = (0, 768, 1024, 1280, N_LIST)
-NARROW = 1024
+CUTS = (0, 512, 768, 1024, 1280, N_LIST)
+TWO_BANKS = (2, 3)
 WARM_UP_WIDTHS = (512, 64)
+
 
 def tile_list_tabbag_tm_none_kernel(tc, tab, w, offs, out):
     nc = tc.nc
@@ -39,9 +40,12 @@ def tile_list_tabbag_tm_none_kernel(tc, tab, w, offs, out):
         reused = ctx.enter_context(tc.tile_pool(name="reused", bufs=1))
         psum = ctx.enter_context(tc.psum_pool(name="psum", bufs=1))
 
-        halves = [(a, n0) for a in range(PASSES) for n0 in (0, HALF)]
-        at_raw = {half: i * RAW_BYTES for i, half in enumerate(halves)}
-        at_scale_rows = RAW_BYTES + RAW_BYTES // 2
+        at_raw0_first = 0
+        at_raw0_second = RAW_BYTES
+        at_scale_rows = 2 * RAW_BYTES
+        at_rounded0_first = at_scale_rows + T
+        at_raw = {(0, 0): at_raw0_first, (0, HALF): at_raw0_second, (1, 0): at_scale_rows, (1, HALF): at_raw0_first}
+        at_piece = (at_raw0_second, at_scale_rows, at_raw0_first, at_raw0_first + RAW_BYTES // 2)
 
         offsets = keep.tile([P, N_LIST // PER_COL], U16, name="offsets")
         scale_rows = reused.tile([P, T], U8, name="scale_rows", offset=at_scale_rows, align_bytes=64)
@@ -49,7 +53,6 @@ def tile_list_tabbag_tm_none_kernel(tc, tab, w, offs, out):
         w_codes = [keep.tile([P, M], U32, name=f"w_codes{a}", align_bytes=64) for a in range(PASSES)]
         w_planes = [keep.tile([P, M], U8, name=f"w_planes{a}", align_bytes=64) for a in range(PASSES)]
         picked_rows = keep.tile([P, N_LIST], U8, name="picked_rows", align_bytes=64)
-        planes = keep.tile([P, PASSES * N_LIST], U8, name="planes", align_bytes=64)
         picked_words = {}
         raw = {}
 
@@ -61,8 +64,7 @@ def tile_list_tabbag_tm_none_kernel(tc, tab, w, offs, out):
             rows = w[a * K_PASS : (a + 1) * K_PASS, :].rearrange("(p t) n -> p t n", t=PACK)
             nc.sync.dma_start(raw[a, n0][:], rows[:, :, n0 : n0 + HALF])
 
-        def quantise_w(a, n0):
-            rounded = keep.tile([P, HALF, PACK], BF16, name=f"rounded{a}_{n0}", align_bytes=64)
+        def quantise_w(a, n0, rounded):
             nc.scalar.copy(
                 rounded[:].rearrange("p (c e) t -> p c t e", e=4),
                 raw[a, n0][:].rearrange("p t (c e) -> p c t e", e=4),
@@ -73,10 +75,10 @@ def tile_list_tabbag_tm_none_kernel(tc, tab, w, offs, out):
                 in_=rounded[:].rearrange("p n t -> p (n t)"),
             )
 
-        def move_to_plane(a, lo, hi):
+        def move_to_plane(plane, a, lo, hi, queue):
             for r in range(LIVE_ROWS):
-                nc.sync.dma_start(
-                    planes[r:P:QUADRANT, a * N_LIST + lo : a * N_LIST + hi].bitcast(I32),
+                queue.dma_start(
+                    plane[r:P:QUADRANT, lo:hi].bitcast(I32),
                     picked_rows[ROW0 + PASSES * r + a : P : PASSES * LIVE_ROWS, lo:hi].bitcast(I32),
                 )
 
@@ -94,30 +96,70 @@ def tile_list_tabbag_tm_none_kernel(tc, tab, w, offs, out):
         load_words(0)
         load_w(0, 0)
         load_words(1)
+        load_w(0, HALF)
 
         nc.vector.memset(scale_rows[0:ROW0, :].bitcast(I32), 0)
-        nc.vector.memset(planes[:].bitcast(I32), 0)
+        plane0 = keep.tile([P, N_LIST], U8, name="plane0", align_bytes=64)
+        nc.vector.memset(plane0[:].bitcast(I32), 0)
         nc.vector.tensor_copy(picked_rows[:], scale_rows[:].indirect(offsets[:]))
-
-        move_to_plane(0, 0, N_LIST)
-        load_w(0, HALF)
+        move_to_plane(plane0, 0, 0, N_LIST, nc.scalar)
         load_w(1, 0)
+
+        picked0 = keep.tile([P, N_LIST], U32, name="picked0", align_bytes=64)
+        gather_words(0, 0, N_LIST, picked0)
+        rounded0_first = reused.tile(
+            [P, HALF, PACK], BF16, name="rounded0_first", offset=at_rounded0_first, align_bytes=64
+        )
+        quantise_w(0, 0, rounded0_first)
         load_w(1, HALF)
-        move_to_plane(1, 0, CUTS[-2])
-        move_to_plane(1, CUTS[-2], N_LIST)
 
-        gather_words(0, 0, N_LIST, keep.tile([P, N_LIST], U32, name="picked0", align_bytes=64))
-        quantise_w(0, 0)
+        plane1 = reused.tile([P, N_LIST], U8, name="plane1", offset=at_rounded0_first, align_bytes=64)
+        nc.vector.memset(plane1[:].bitcast(I32), 0)
+        move_to_plane(plane1, 1, 0, CUTS[-2], nc.sync)
+        move_to_plane(plane1, 1, CUTS[-2], N_LIST, nc.sync)
+        planes = (plane0, plane1)
 
-        for i in range(len(CUTS) - 1):
+        gather_words(1, CUTS[0], CUTS[1], keep.tile([P, CUTS[1]], U32, name="picked1_0", align_bytes=64))
+        late_halves = ((0, HALF), (1, 0), (1, HALF))
+        for i in range(1, len(CUTS) - 1):
+            if i <= len(late_halves):
+                a, n0 = late_halves[i - 1]
+                quantise_w(a, n0, keep.tile([P, HALF, PACK], BF16, name=f"rounded{a}_{n0}", align_bytes=64))
             lo, hi = CUTS[i], CUTS[i + 1]
-            if i == 0:
-                piece = keep.tile([P, hi - lo], U32, name="picked1_0", align_bytes=64)
-            else:
-                piece = reused.tile([P, hi - lo], U32, name=f"picked1_{i}", offset=at_raw[halves[i]], align_bytes=64)
+            piece = reused.tile([P, hi - lo], U32, name=f"picked1_{i}", offset=at_piece[i - 1], align_bytes=64)
             gather_words(1, lo, hi, piece)
-            if i + 1 < len(halves):
-                quantise_w(*halves[i + 1])
+
+        banks = {}
+        for j in range(ROW_BLOCKS):
+            if j in TWO_BANKS:
+                for n0 in (0, HALF):
+                    banks[j, n0] = (psum.tile([P, HALF], F32, name=f"acc{j}_{n0}"), n0)
+            else:
+                banks[j, 0] = banks[j, HALF] = (psum.tile([P, M], F32, name=f"acc{j}"), 0)
+
+        def multiply(a, g, j, n0, n1):
+            if j in TWO_BANKS and n1 - n0 == M:
+                multiply(a, g, j, 0, HALF)
+                multiply(a, g, j, HALF, M)
+                return
+            bank, bank_col = banks[j, n0]
+            m = g * S + j * P
+            nc.tensor.matmul_mx(
+                out=bank[:, n0 - bank_col : n1 - bank_col],
+                lhsT=picked_words[a, m].bitcast(FP8X4),
+                lhsT_scale=planes[a][:, m : m + P],
+                rhs=w_codes[a][:, n0:n1].bitcast(FP8X4),
+                rhs_scale=w_planes[a][:, n0:n1],
+                start=(a == 0 and g == 0 and n0 == bank_col),
+                stop=(a == PASSES - 1 and g == G - 1),
+            )
+
+        def multiply_half(a, n0, list_rows):
+            for g in list_rows:
+                for j in range(ROW_BLOCKS):
+                    multiply(a, g, j, n0, n0 + HALF)
+
+        multiply_half(0, 0, range(G))
 
         for width in WARM_UP_WIDTHS:
             unread = psum.tile([P, width], F32, name=f"unread{width}")
@@ -125,57 +167,24 @@ def tile_list_tabbag_tm_none_kernel(tc, tab, w, offs, out):
                 out=unread[:],
                 lhsT=w_codes[0][:, 0:HALF].bitcast(FP8X4),
                 lhsT_scale=w_planes[0][:, 0:HALF],
-                rhs=tab_words[1][:, 0:width].bitcast(FP8X4),
-                rhs_scale=picked_rows[:, 0:width],
+                rhs=picked0[:, 0:width].bitcast(FP8X4),
+                rhs_scale=plane0[:, 0:width],
                 start=True,
                 stop=True,
             )
 
-        last = ROW_BLOCKS - 1
-        banks = {}
-        for j in range(last):
-            banks[j, 0] = banks[j, HALF] = (psum.tile([P, M], F32, name=f"acc{j}"), 0)
-        for n0 in (0, HALF):
-            banks[last, n0] = (psum.tile([P, HALF], F32, name=f"acc{last}_{n0}"), n0)
-
-        def multiply(a, m, n0, n1):
-            g, j = m // S, m % S // P
-            if j == last and n1 - n0 == M:
-                multiply(a, m, 0, HALF)
-                multiply(a, m, HALF, M)
-                return
-            bank, bank_col = banks[j, n0]
-            nc.tensor.matmul_mx(
-                out=bank[:, n0 - bank_col : n1 - bank_col],
-                lhsT=picked_words[a, m].bitcast(FP8X4),
-                lhsT_scale=planes[:, a * N_LIST + m : a * N_LIST + m + P],
-                rhs=w_codes[a][:, n0:n1].bitcast(FP8X4),
-                rhs_scale=w_planes[a][:, n0:n1],
-                start=(a == 0 and g == 0 and n0 == bank_col),
-                stop=(a == PASSES - 1 and g == G - 1 and (n1 == M or j == last)),
-            )
-
-        for n0 in (0, HALF):
-            for m in range(0, N_LIST, P):
-                multiply(0, m, n0, n0 + HALF)
-        for m in range(0, NARROW, P):
-            multiply(1, m, 0, HALF)
+        multiply_half(0, HALF, range(G))
+        multiply_half(1, 0, range(G - 1))
         for j in range(ROW_BLOCKS):
-            if j == last:
-                multiply(1, N_LIST - P, 0, HALF)
-            for m in range(j * P, N_LIST, S):
-                multiply(1, m, HALF if m < NARROW or j == last else 0, M)
+            for g in range(G - 1):
+                multiply(1, g, j, HALF, M)
+            multiply(1, G - 1, j, 0, M)
 
-        results = reused.tile(
-            [P, ROW_BLOCKS * M], F32, name="results", offset=at_raw[halves[-1]] + RAW_BYTES // 2, align_bytes=64
-        )
         for j in range(ROW_BLOCKS):
-            result = results[:, j * M : (j + 1) * M]
-            if j == last:
-                for n0 in (0, HALF):
-                    nc.vector.tensor_copy(result[:, n0 : n0 + HALF], banks[j, n0][0][:])
-            elif j % 2 == 0:
-                nc.scalar.copy(result, banks[j, 0][0][:])
+            result = keep.tile([P, M], F32, name=f"result{j}")
+            if j in TWO_BANKS:
+                nc.scalar.copy(result[:, 0:HALF], banks[j, 0][0][:])
+                nc.vector.tensor_copy(result[:, HALF:M], banks[j, HALF][0][:])
             else:
-                nc.vector.tensor_copy(result, banks[j, 0][0][:])
-            nc.sync.dma_start(out[j * P : (j + 1) * P, :], result)
+                nc.scalar.copy(result[:], banks[j, 0][0][:])
+            nc.sync.dma_start(out[j * P : (j + 1) * P, :], result[:])

@@ -28,7 +28,8 @@ HALF = M // 2
 ROW0 = P - PASSES * BLOCKS
 RAW_BYTES = PACK * HALF * 4
 
-CUTS = (0, 512, 768, 1024, 1280, N_LIST)
+LATE_WORDS = T - T // 4
+CUTS = (0, 640, 1024, 1280, N_LIST)
 TWO_BANKS = (2, 3)
 WARM_UP_WIDTHS = (512, 64)
 
@@ -40,24 +41,22 @@ def tile_list_tabbag_tm_none_kernel(tc, tab, w, offs, out):
         reused = ctx.enter_context(tc.tile_pool(name="reused", bufs=1))
         psum = ctx.enter_context(tc.psum_pool(name="psum", bufs=1))
 
-        at_raw0_first = 0
-        at_raw0_second = RAW_BYTES
-        at_scale_rows = 2 * RAW_BYTES
-        at_rounded0_first = at_scale_rows + T
-        at_raw = {(0, 0): at_raw0_first, (0, HALF): at_raw0_second, (1, 0): at_scale_rows, (1, HALF): at_raw0_first}
-        at_piece = (at_raw0_second, at_scale_rows, at_raw0_first, at_raw0_first + RAW_BYTES // 2)
+        at_raw = {(0, 0): RAW_BYTES // 2, (0, HALF): 0, (1, 0): RAW_BYTES, (1, HALF): 2 * RAW_BYTES}
+        at_plane1 = 3 * RAW_BYTES
+        at_rounded0_first = at_plane1 - RAW_BYTES // 4
 
         offsets = keep.tile([P, N_LIST // PER_COL], U16, name="offsets")
-        scale_rows = reused.tile([P, T], U8, name="scale_rows", offset=at_scale_rows, align_bytes=64)
         tab_words = [keep.tile([P, T], I32, name=f"tab_words{a}", align_bytes=64) for a in range(PASSES)]
+        scale_rows = tab_words[1][:, LATE_WORDS:T]
         w_codes = [keep.tile([P, M], U32, name=f"w_codes{a}", align_bytes=64) for a in range(PASSES)]
         w_planes = [keep.tile([P, M], U8, name=f"w_planes{a}", align_bytes=64) for a in range(PASSES)]
         picked_rows = keep.tile([P, N_LIST], U8, name="picked_rows", align_bytes=64)
         picked_words = {}
         raw = {}
 
-        def load_words(a):
-            nc.sync.dma_start(tab_words[a][:], tab[a, 0:WORD_BYTES].rearrange("(p b) -> p b", p=P).bitcast(I32))
+        def load_words(a, t0, t1):
+            words = tab[a, 0:WORD_BYTES].rearrange("(p b) -> p b", p=P).bitcast(I32)
+            nc.sync.dma_start(tab_words[a][:, t0:t1], words[:, t0:t1])
 
         def load_w(a, n0):
             raw[a, n0] = reused.tile([P, PACK, HALF], F32, name=f"raw{a}_{n0}", offset=at_raw[a, n0], align_bytes=64)
@@ -75,11 +74,11 @@ def tile_list_tabbag_tm_none_kernel(tc, tab, w, offs, out):
                 in_=rounded[:].rearrange("p n t -> p (n t)"),
             )
 
-        def move_to_plane(plane, a, lo, hi, queue):
+        def move_to_plane(plane, a):
             for r in range(LIVE_ROWS):
-                queue.dma_start(
-                    plane[r:P:QUADRANT, lo:hi].bitcast(I32),
-                    picked_rows[ROW0 + PASSES * r + a : P : PASSES * LIVE_ROWS, lo:hi].bitcast(I32),
+                nc.sync.dma_start(
+                    plane[r:P:QUADRANT, :].bitcast(I32),
+                    picked_rows[ROW0 + PASSES * r + a : P : PASSES * LIVE_ROWS, :].bitcast(I32),
                 )
 
         def gather_words(a, lo, hi, picked):
@@ -89,21 +88,20 @@ def tile_list_tabbag_tm_none_kernel(tc, tab, w, offs, out):
                 picked_words[a, m] = picked[:, m - lo : m - lo + P]
 
         nc.sync.dma_start(
-            scale_rows[ROW0:P, :].bitcast(I32),
+            scale_rows[ROW0:P, :],
             tab[:, WORD_BYTES : WORD_BYTES + BLOCKS * T].rearrange("a (q t) -> q a t", q=BLOCKS).bitcast(I32),
         )
         nc.sync.dma_start(offsets[:], offs)
-        load_words(0)
+        load_words(0, 0, T)
         load_w(0, 0)
-        load_words(1)
-        load_w(0, HALF)
+        load_words(1, 0, LATE_WORDS)
 
-        nc.vector.memset(scale_rows[0:ROW0, :].bitcast(I32), 0)
+        nc.vector.memset(scale_rows[0:ROW0, :], 0)
         plane0 = keep.tile([P, N_LIST], U8, name="plane0", align_bytes=64)
         nc.vector.memset(plane0[:].bitcast(I32), 0)
-        nc.vector.tensor_copy(picked_rows[:], scale_rows[:].indirect(offsets[:]))
-        move_to_plane(plane0, 0, 0, N_LIST, nc.scalar)
-        load_w(1, 0)
+        nc.vector.tensor_copy(picked_rows[:], scale_rows.bitcast(U8).indirect(offsets[:]))
+        move_to_plane(plane0, 0)
+        load_words(1, LATE_WORDS, T)
 
         picked0 = keep.tile([P, N_LIST], U32, name="picked0", align_bytes=64)
         gather_words(0, 0, N_LIST, picked0)
@@ -111,22 +109,22 @@ def tile_list_tabbag_tm_none_kernel(tc, tab, w, offs, out):
             [P, HALF, PACK], BF16, name="rounded0_first", offset=at_rounded0_first, align_bytes=64
         )
         quantise_w(0, 0, rounded0_first)
+        load_w(0, HALF)
+        load_w(1, 0)
         load_w(1, HALF)
 
-        plane1 = reused.tile([P, N_LIST], U8, name="plane1", offset=at_rounded0_first, align_bytes=64)
+        plane1 = reused.tile([P, N_LIST], U8, name="plane1", offset=at_plane1, align_bytes=64)
         nc.vector.memset(plane1[:].bitcast(I32), 0)
-        move_to_plane(plane1, 1, 0, CUTS[-2], nc.sync)
-        move_to_plane(plane1, 1, CUTS[-2], N_LIST, nc.sync)
+        move_to_plane(plane1, 1)
         planes = (plane0, plane1)
 
         gather_words(1, CUTS[0], CUTS[1], keep.tile([P, CUTS[1]], U32, name="picked1_0", align_bytes=64))
         late_halves = ((0, HALF), (1, 0), (1, HALF))
         for i in range(1, len(CUTS) - 1):
-            if i <= len(late_halves):
-                a, n0 = late_halves[i - 1]
-                quantise_w(a, n0, keep.tile([P, HALF, PACK], BF16, name=f"rounded{a}_{n0}", align_bytes=64))
+            a, n0 = late_halves[i - 1]
+            quantise_w(a, n0, keep.tile([P, HALF, PACK], BF16, name=f"rounded{a}_{n0}", align_bytes=64))
             lo, hi = CUTS[i], CUTS[i + 1]
-            piece = reused.tile([P, hi - lo], U32, name=f"picked1_{i}", offset=at_piece[i - 1], align_bytes=64)
+            piece = reused.tile([P, hi - lo], U32, name=f"picked1_{i}", offset=at_raw[a, n0], align_bytes=64)
             gather_words(1, lo, hi, piece)
 
         banks = {}
@@ -138,10 +136,6 @@ def tile_list_tabbag_tm_none_kernel(tc, tab, w, offs, out):
                 banks[j, 0] = banks[j, HALF] = (psum.tile([P, M], F32, name=f"acc{j}"), 0)
 
         def multiply(a, g, j, n0, n1):
-            if j in TWO_BANKS and n1 - n0 == M:
-                multiply(a, g, j, 0, HALF)
-                multiply(a, g, j, HALF, M)
-                return
             bank, bank_col = banks[j, n0]
             m = g * S + j * P
             nc.tensor.matmul_mx(
@@ -159,32 +153,35 @@ def tile_list_tabbag_tm_none_kernel(tc, tab, w, offs, out):
                 for j in range(ROW_BLOCKS):
                     multiply(a, g, j, n0, n0 + HALF)
 
-        multiply_half(0, 0, range(G))
-
         for width in WARM_UP_WIDTHS:
             unread = psum.tile([P, width], F32, name=f"unread{width}")
             nc.tensor.matmul_mx(
                 out=unread[:],
                 lhsT=w_codes[0][:, 0:HALF].bitcast(FP8X4),
                 lhsT_scale=w_planes[0][:, 0:HALF],
-                rhs=picked0[:, 0:width].bitcast(FP8X4),
-                rhs_scale=plane0[:, 0:width],
+                rhs=tab_words[1][:, 0:width].bitcast(FP8X4),
+                rhs_scale=picked_rows[:, 0:width],
                 start=True,
                 stop=True,
             )
 
+        multiply_half(0, 0, range(G))
         multiply_half(0, HALF, range(G))
         multiply_half(1, 0, range(G - 1))
         for j in range(ROW_BLOCKS):
+            if j in TWO_BANKS:
+                multiply(1, G - 1, j, 0, HALF)
             for g in range(G - 1):
                 multiply(1, g, j, HALF, M)
-            multiply(1, G - 1, j, 0, M)
+            multiply(1, G - 1, j, HALF if j in TWO_BANKS else 0, M)
 
+        parts = []
         for j in range(ROW_BLOCKS):
-            result = keep.tile([P, M], F32, name=f"result{j}")
-            if j in TWO_BANKS:
-                nc.scalar.copy(result[:, 0:HALF], banks[j, 0][0][:])
-                nc.vector.tensor_copy(result[:, HALF:M], banks[j, HALF][0][:])
+            parts.extend([(j, 0, HALF), (j, HALF, M)] if j in TWO_BANKS else [(j, 0, M)])
+        for i, (j, n0, n1) in enumerate(parts):
+            result = keep.tile([P, n1 - n0], F32, name=f"result{j}_{n0}")
+            if i % 2 == 0:
+                nc.scalar.copy(result[:], banks[j, n0][0][:])
             else:
-                nc.scalar.copy(result[:], banks[j, 0][0][:])
-            nc.sync.dma_start(out[j * P : (j + 1) * P, :], result[:])
+                nc.vector.tensor_copy(result[:], banks[j, n0][0][:])
+            nc.sync.dma_start(out[j * P : (j + 1) * P, n0:n1], result[:])

@@ -28,9 +28,10 @@ HALF = M // 2
 ROW0 = P - PASSES * BLOCKS
 RAW_BYTES = PACK * HALF * 4
 
-LATE_WORDS = T - T // 4
-CUTS = (0, 640, 1024, 1280, N_LIST)
-TWO_BANKS = (2, 3)
+CUTS = (0, 768, 1024, 1280, N_LIST)
+NARROW = 1152
+HALF_FIRST = 2
+LAST = ROW_BLOCKS - 1
 WARM_UP_WIDTHS = (512, 64)
 
 
@@ -47,16 +48,15 @@ def tile_list_tabbag_tm_none_kernel(tc, tab, w, offs, out):
 
         offsets = keep.tile([P, N_LIST // PER_COL], U16, name="offsets")
         tab_words = [keep.tile([P, T], I32, name=f"tab_words{a}", align_bytes=64) for a in range(PASSES)]
-        scale_rows = tab_words[1][:, LATE_WORDS:T]
+        scale_rows = keep.tile([P, T], U8, name="scale_rows", align_bytes=64)
         w_codes = [keep.tile([P, M], U32, name=f"w_codes{a}", align_bytes=64) for a in range(PASSES)]
         w_planes = [keep.tile([P, M], U8, name=f"w_planes{a}", align_bytes=64) for a in range(PASSES)]
         picked_rows = keep.tile([P, N_LIST], U8, name="picked_rows", align_bytes=64)
         picked_words = {}
         raw = {}
 
-        def load_words(a, t0, t1):
-            words = tab[a, 0:WORD_BYTES].rearrange("(p b) -> p b", p=P).bitcast(I32)
-            nc.sync.dma_start(tab_words[a][:, t0:t1], words[:, t0:t1])
+        def load_words(a):
+            nc.sync.dma_start(tab_words[a][:], tab[a, 0:WORD_BYTES].rearrange("(p b) -> p b", p=P).bitcast(I32))
 
         def load_w(a, n0):
             raw[a, n0] = reused.tile([P, PACK, HALF], F32, name=f"raw{a}_{n0}", offset=at_raw[a, n0], align_bytes=64)
@@ -74,11 +74,11 @@ def tile_list_tabbag_tm_none_kernel(tc, tab, w, offs, out):
                 in_=rounded[:].rearrange("p n t -> p (n t)"),
             )
 
-        def move_to_plane(plane, a):
+        def move_to_plane(plane, a, lo, hi):
             for r in range(LIVE_ROWS):
                 nc.sync.dma_start(
-                    plane[r:P:QUADRANT, :].bitcast(I32),
-                    picked_rows[ROW0 + PASSES * r + a : P : PASSES * LIVE_ROWS, :].bitcast(I32),
+                    plane[r:P:QUADRANT, lo:hi].bitcast(I32),
+                    picked_rows[ROW0 + PASSES * r + a : P : PASSES * LIVE_ROWS, lo:hi].bitcast(I32),
                 )
 
         def gather_words(a, lo, hi, picked):
@@ -88,20 +88,19 @@ def tile_list_tabbag_tm_none_kernel(tc, tab, w, offs, out):
                 picked_words[a, m] = picked[:, m - lo : m - lo + P]
 
         nc.sync.dma_start(
-            scale_rows[ROW0:P, :],
+            scale_rows[ROW0:P, :].bitcast(I32),
             tab[:, WORD_BYTES : WORD_BYTES + BLOCKS * T].rearrange("a (q t) -> q a t", q=BLOCKS).bitcast(I32),
         )
         nc.sync.dma_start(offsets[:], offs)
-        load_words(0, 0, T)
+        load_words(0)
         load_w(0, 0)
-        load_words(1, 0, LATE_WORDS)
+        load_words(1)
 
-        nc.vector.memset(scale_rows[0:ROW0, :], 0)
+        nc.vector.memset(scale_rows[0:ROW0, :].bitcast(I32), 0)
         plane0 = keep.tile([P, N_LIST], U8, name="plane0", align_bytes=64)
         nc.vector.memset(plane0[:].bitcast(I32), 0)
-        nc.vector.tensor_copy(picked_rows[:], scale_rows.bitcast(U8).indirect(offsets[:]))
-        move_to_plane(plane0, 0)
-        load_words(1, LATE_WORDS, T)
+        nc.vector.tensor_copy(picked_rows[:], scale_rows[:].indirect(offsets[:]))
+        move_to_plane(plane0, 0, 0, N_LIST)
 
         picked0 = keep.tile([P, N_LIST], U32, name="picked0", align_bytes=64)
         gather_words(0, 0, N_LIST, picked0)
@@ -115,29 +114,38 @@ def tile_list_tabbag_tm_none_kernel(tc, tab, w, offs, out):
 
         plane1 = reused.tile([P, N_LIST], U8, name="plane1", offset=at_plane1, align_bytes=64)
         nc.vector.memset(plane1[:].bitcast(I32), 0)
-        move_to_plane(plane1, 1)
+        move_to_plane(plane1, 1, 0, CUTS[-2])
+        move_to_plane(plane1, 1, CUTS[-2], N_LIST)
         planes = (plane0, plane1)
 
-        gather_words(1, CUTS[0], CUTS[1], keep.tile([P, CUTS[1]], U32, name="picked1_0", align_bytes=64))
-        late_halves = ((0, HALF), (1, 0), (1, HALF))
-        for i in range(1, len(CUTS) - 1):
-            a, n0 = late_halves[i - 1]
-            quantise_w(a, n0, keep.tile([P, HALF, PACK], BF16, name=f"rounded{a}_{n0}", align_bytes=64))
+        def gather_piece(i, at):
             lo, hi = CUTS[i], CUTS[i + 1]
-            piece = reused.tile([P, hi - lo], U32, name=f"picked1_{i}", offset=at_raw[a, n0], align_bytes=64)
-            gather_words(1, lo, hi, piece)
+            gather_words(1, lo, hi, reused.tile([P, hi - lo], U32, name=f"picked1_{i}", offset=at, align_bytes=64))
+
+        gather_words(1, CUTS[0], CUTS[1], keep.tile([P, CUTS[1]], U32, name="picked1_0", align_bytes=64))
+        quantise_w(0, HALF, keep.tile([P, HALF, PACK], BF16, name="rounded0_second", align_bytes=64))
+        gather_piece(1, at_raw[0, HALF])
+        for n0 in (0, HALF):
+            quantise_w(1, n0, keep.tile([P, HALF, PACK], BF16, name=f"rounded1_{n0}", align_bytes=64))
+        gather_piece(2, at_raw[1, HALF])
+        gather_piece(3, at_raw[1, HALF] + RAW_BYTES // 2)
 
         banks = {}
         for j in range(ROW_BLOCKS):
-            if j in TWO_BANKS:
+            if j == LAST:
                 for n0 in (0, HALF):
                     banks[j, n0] = (psum.tile([P, HALF], F32, name=f"acc{j}_{n0}"), n0)
             else:
                 banks[j, 0] = banks[j, HALF] = (psum.tile([P, M], F32, name=f"acc{j}"), 0)
 
+        passes_left = {}
+        for (j, n0), (bank, bank_col) in banks.items():
+            passes_left[j, bank_col] = passes_left.get((j, bank_col), 0) + PASSES * G * HALF
+
         def multiply(a, g, j, n0, n1):
             bank, bank_col = banks[j, n0]
             m = g * S + j * P
+            passes_left[j, bank_col] -= n1 - n0
             nc.tensor.matmul_mx(
                 out=bank[:, n0 - bank_col : n1 - bank_col],
                 lhsT=picked_words[a, m].bitcast(FP8X4),
@@ -145,13 +153,8 @@ def tile_list_tabbag_tm_none_kernel(tc, tab, w, offs, out):
                 rhs=w_codes[a][:, n0:n1].bitcast(FP8X4),
                 rhs_scale=w_planes[a][:, n0:n1],
                 start=(a == 0 and g == 0 and n0 == bank_col),
-                stop=(a == PASSES - 1 and g == G - 1),
+                stop=(passes_left[j, bank_col] == 0),
             )
-
-        def multiply_half(a, n0, list_rows):
-            for g in list_rows:
-                for j in range(ROW_BLOCKS):
-                    multiply(a, g, j, n0, n0 + HALF)
 
         for width in WARM_UP_WIDTHS:
             unread = psum.tile([P, width], F32, name=f"unread{width}")
@@ -165,23 +168,38 @@ def tile_list_tabbag_tm_none_kernel(tc, tab, w, offs, out):
                 stop=True,
             )
 
-        multiply_half(0, 0, range(G))
-        multiply_half(0, HALF, range(G))
-        multiply_half(1, 0, range(G - 1))
-        for j in range(ROW_BLOCKS):
-            if j in TWO_BANKS:
-                multiply(1, G - 1, j, 0, HALF)
+        def multiply_whole(a, g, j):
+            if j == LAST:
+                multiply(a, g, j, 0, HALF)
+                multiply(a, g, j, HALF, M)
+            else:
+                multiply(a, g, j, 0, M)
+
+        pairs = [(g, j) for g in range(G) for j in range(ROW_BLOCKS)]
+        for n0 in (0, HALF):
+            for g, j in pairs[: NARROW // P]:
+                multiply(0, g, j, n0, n0 + HALF)
+        for g, j in pairs[NARROW // P :]:
+            multiply_whole(0, g, j)
+
+        for j in range(HALF_FIRST):
             for g in range(G - 1):
-                multiply(1, g, j, HALF, M)
-            multiply(1, G - 1, j, HALF if j in TWO_BANKS else 0, M)
+                multiply(1, g, j, 0, HALF)
+        for j in range(LAST):
+            for g in range(G):
+                multiply(1, g, j, HALF if j < HALF_FIRST and g < G - 1 else 0, M)
+        for n0 in (0, HALF):
+            for g in reversed(range(G)):
+                multiply(1, g, LAST, n0, n0 + HALF)
 
         parts = []
         for j in range(ROW_BLOCKS):
-            parts.extend([(j, 0, HALF), (j, HALF, M)] if j in TWO_BANKS else [(j, 0, M)])
-        for i, (j, n0, n1) in enumerate(parts):
-            result = keep.tile([P, n1 - n0], F32, name=f"result{j}_{n0}")
-            if i % 2 == 0:
-                nc.scalar.copy(result[:], banks[j, n0][0][:])
+            parts.extend([(j, 0, HALF), (j, HALF, M)] if j == LAST else [(j, 0, M)])
+        results = [keep.tile([P, M], F32, name=f"result{j}") for j in range(ROW_BLOCKS)]
+        for j, n0, n1 in parts:
+            if j != LAST - 1:
+                nc.scalar.copy(results[j][:, n0:n1], banks[j, n0][0][:])
             else:
-                nc.vector.tensor_copy(result[:], banks[j, n0][0][:])
-            nc.sync.dma_start(out[j * P : (j + 1) * P, n0:n1], result[:])
+                nc.vector.tensor_copy(results[j][:, n0:n1], banks[j, n0][0][:])
+            if n1 == M:
+                nc.sync.dma_start(out[j * P : (j + 1) * P, :], results[j][:])

@@ -32,7 +32,6 @@ CUTS = (0, 768, 1024, 1280, N_LIST)
 NARROW = 1152
 HALF_FIRST = 2
 LAST = ROW_BLOCKS - 1
-WARM_UP_WIDTHS = (512, 64)
 
 
 def tile_list_tabbag_tm_none_kernel(tc, tab, w, offs, out):
@@ -154,18 +153,6 @@ def tile_list_tabbag_tm_none_kernel(tc, tab, w, offs, out):
                 rhs_scale=w_planes[a][:, n0:n1],
                 start=(a == 0 and g == 0 and n0 == bank_col),
                 stop=(passes_left[j, bank_col] == 0),
-            )
-
-        for width in WARM_UP_WIDTHS:
-            unread = psum.tile([P, width], F32, name=f"unread{width}")
-            nc.tensor.matmul_mx(
-                out=unread[:],
-                lhsT=w_codes[0][:, 0:HALF].bitcast(FP8X4),
-                lhsT_scale=w_planes[0][:, 0:HALF],
-                rhs=tab_words[1][:, 0:width].bitcast(FP8X4),
-                rhs_scale=picked_rows[:, 0:width],
-                start=True,
-                stop=True,
             )
 
         def multiply_whole(a, g, j):

from contextlib import ExitStack

import concourse.mybir as mybir

G, K, M, T, S = 3, 1024, 256, 4096, 512
FLOPS = 2 * G * K * M * S

F32 = mybir.dt.float32
BF16 = mybir.dt.bfloat16
I32 = mybir.dt.int32
U32 = mybir.dt.uint32
U16 = mybir.dt.uint16
U8 = mybir.dt.uint8
FP8X4 = mybir.dt.float8_e4m3fn_x4

P = 128
PACK = 4
K_PASS = P * PACK
PASSES = K // K_PASS
N_LIST = G * S
ROW_BLOCKS = S // P
PER_COL = 16
WORD_BYTES = K_PASS * T
BLOCKS = K_PASS // 32
QUADRANT = 32
LIVE_ROWS = 4
HALF = M // 2
ROW0 = P - PASSES * BLOCKS
RAW_BYTES = PACK * HALF * 4

CUTS = (0, 768, 1024, 1280, N_LIST)
NARROW = 1152
HALF_FIRST = 2
LAST = ROW_BLOCKS - 1


def tile_list_tabbag_tm_none_kernel(tc, tab, w, offs, out):
    nc = tc.nc
    with ExitStack() as ctx:
        keep = ctx.enter_context(tc.tile_pool(name="keep", bufs=1))
        reused = ctx.enter_context(tc.tile_pool(name="reused", bufs=1))
        psum = ctx.enter_context(tc.psum_pool(name="psum", bufs=1))

        at_raw = {(0, 0): RAW_BYTES // 2, (0, HALF): 0, (1, 0): RAW_BYTES, (1, HALF): 2 * RAW_BYTES}
        at_plane1 = 3 * RAW_BYTES
        at_rounded0_first = at_plane1 - RAW_BYTES // 4

        offsets = keep.tile([P, N_LIST // PER_COL], U16, name="offsets")
        tab_words = [keep.tile([P, T], I32, name=f"tab_words{a}", align_bytes=64) for a in range(PASSES)]
        scale_rows = keep.tile([P, T], U8, name="scale_rows", align_bytes=64)
        w_codes = [keep.tile([P, M], U32, name=f"w_codes{a}", align_bytes=64) for a in range(PASSES)]
        w_planes = [keep.tile([P, M], U8, name=f"w_planes{a}", align_bytes=64) for a in range(PASSES)]
        picked_rows = keep.tile([P, N_LIST], U8, name="picked_rows", align_bytes=64)
        picked_words = {}
        raw = {}

        def load_words(a):
            nc.sync.dma_start(tab_words[a][:], tab[a, 0:WORD_BYTES].rearrange("(p b) -> p b", p=P).bitcast(I32))

        def load_w(a, n0):
            raw[a, n0] = reused.tile([P, PACK, HALF], F32, name=f"raw{a}_{n0}", offset=at_raw[a, n0], align_bytes=64)
            rows = w[a * K_PASS : (a + 1) * K_PASS, :].rearrange("(p t) n -> p t n", t=PACK)
            nc.sync.dma_start(raw[a, n0][:], rows[:, :, n0 : n0 + HALF])

        def quantise_w(a, n0, rounded):
            nc.scalar.copy(
                rounded[:].rearrange("p (c e) t -> p c t e", e=4),
                raw[a, n0][:].rearrange("p t (c e) -> p c t e", e=4),
            )
            nc.vector.quantize_mx(
                out=w_codes[a][:, n0 : n0 + HALF].bitcast(FP8X4),
                scales=w_planes[a][:, n0 : n0 + HALF],
                in_=rounded[:].rearrange("p n t -> p (n t)"),
            )

        def move_to_plane(plane, a, lo, hi):
            for r in range(LIVE_ROWS):
                nc.sync.dma_start(
                    plane[r:P:QUADRANT, lo:hi].bitcast(I32),
                    picked_rows[ROW0 + PASSES * r + a : P : PASSES * LIVE_ROWS, lo:hi].bitcast(I32),
                )

        def gather_words(a, lo, hi, picked):
            window = tab_words[a][:].bitcast(U32)
            nc.vector.tensor_copy(picked[:], window.indirect(offsets[:, lo // PER_COL : hi // PER_COL]))
            for m in range(lo, hi, P):
                picked_words[a, m] = picked[:, m - lo : m - lo + P]

        nc.sync.dma_start(
            scale_rows[ROW0:P, :].bitcast(I32),
            tab[:, WORD_BYTES : WORD_BYTES + BLOCKS * T].rearrange("a (q t) -> q a t", q=BLOCKS).bitcast(I32),
        )
        nc.sync.dma_start(offsets[:], offs)
        load_words(0)
        load_w(0, 0)
        load_words(1)

        nc.vector.memset(scale_rows[0:ROW0, :].bitcast(I32), 0)
        plane0 = keep.tile([P, N_LIST], U8, name="plane0", align_bytes=64)
        nc.vector.memset(plane0[:].bitcast(I32), 0)
        nc.vector.tensor_copy(picked_rows[:], scale_rows[:].indirect(offsets[:]))
        move_to_plane(plane0, 0, 0, N_LIST)

        picked0 = keep.tile([P, N_LIST], U32, name="picked0", align_bytes=64)
        gather_words(0, 0, N_LIST, picked0)
        rounded0_first = reused.tile(
            [P, HALF, PACK], BF16, name="rounded0_first", offset=at_rounded0_first, align_bytes=64
        )
        quantise_w(0, 0, rounded0_first)
        load_w(0, HALF)
        load_w(1, 0)
        load_w(1, HALF)

        plane1 = reused.tile([P, N_LIST], U8, name="plane1", offset=at_plane1, align_bytes=64)
        nc.vector.memset(plane1[:].bitcast(I32), 0)
        move_to_plane(plane1, 1, 0, CUTS[-2])
        move_to_plane(plane1, 1, CUTS[-2], N_LIST)
        planes = (plane0, plane1)

        def gather_piece(i, at):
            lo, hi = CUTS[i], CUTS[i + 1]
            gather_words(1, lo, hi, reused.tile([P, hi - lo], U32, name=f"picked1_{i}", offset=at, align_bytes=64))

        gather_words(1, CUTS[0], CUTS[1], keep.tile([P, CUTS[1]], U32, name="picked1_0", align_bytes=64))
        quantise_w(0, HALF, keep.tile([P, HALF, PACK], BF16, name="rounded0_second", align_bytes=64))
        gather_piece(1, at_raw[0, HALF])
        for n0 in (0, HALF):
            quantise_w(1, n0, keep.tile([P, HALF, PACK], BF16, name=f"rounded1_{n0}", align_bytes=64))
        gather_piece(2, at_raw[1, HALF])
        gather_piece(3, at_raw[1, HALF] + RAW_BYTES // 2)

        banks = {}
        for j in range(ROW_BLOCKS):
            if j == LAST:
                for n0 in (0, HALF):
                    banks[j, n0] = (psum.tile([P, HALF], F32, name=f"acc{j}_{n0}"), n0)
            else:
                banks[j, 0] = banks[j, HALF] = (psum.tile([P, M], F32, name=f"acc{j}"), 0)

        passes_left = {}
        for (j, n0), (bank, bank_col) in banks.items():
            passes_left[j, bank_col] = passes_left.get((j, bank_col), 0) + PASSES * G * HALF

        def multiply(a, g, j, n0, n1):
            bank, bank_col = banks[j, n0]
            m = g * S + j * P
            passes_left[j, bank_col] -= n1 - n0
            nc.tensor.matmul_mx(
                out=bank[:, n0 - bank_col : n1 - bank_col],
                lhsT=picked_words[a, m].bitcast(FP8X4),
                lhsT_scale=planes[a][:, m : m + P],
                rhs=w_codes[a][:, n0:n1].bitcast(FP8X4),
                rhs_scale=w_planes[a][:, n0:n1],
                start=(a == 0 and g == 0 and n0 == bank_col),
                stop=(passes_left[j, bank_col] == 0),
            )

        def multiply_whole(a, g, j):
            if j == LAST:
                multiply(a, g, j, 0, HALF)
                multiply(a, g, j, HALF, M)
            else:
                multiply(a, g, j, 0, M)

        pairs = [(g, j) for g in range(G) for j in range(ROW_BLOCKS)]
        for n0 in (0, HALF):
            for g, j in pairs[: NARROW // P]:
                multiply(0, g, j, n0, n0 + HALF)
        for g, j in pairs[NARROW // P :]:
            multiply_whole(0, g, j)

        for j in range(HALF_FIRST):
            for g in range(G - 1):
                multiply(1, g, j, 0, HALF)
        for j in range(LAST):
            for g in range(G):
                multiply(1, g, j, HALF if j < HALF_FIRST and g < G - 1 else 0, M)
        for n0 in (0, HALF):
            for g in reversed(range(G)):
                multiply(1, g, LAST, n0, n0 + HALF)

        parts = []
        for j in range(ROW_BLOCKS):
            parts.extend([(j, 0, HALF), (j, HALF, M)] if j == LAST else [(j, 0, M)])
        results = [keep.tile([P, M], F32, name=f"result{j}") for j in range(ROW_BLOCKS)]
        for j, n0, n1 in parts:
            if j != LAST - 1:
                nc.scalar.copy(results[j][:, n0:n1], banks[j, n0][0][:])
            else:
                nc.vector.tensor_copy(results[j][:, n0:n1], banks[j, n0][0][:])
            if n1 == M:
                nc.sync.dma_start(out[j * P : (j + 1) * P, :], results[j][:])
